import numpy as np
import ml_dtypes


def mxq(x, axis, fmt="e4m3"):
    dtype, down = {"e4m3": (ml_dtypes.float8_e4m3fn, 7), "e5m2": (ml_dtypes.float8_e5m2, 14)}[fmt]
    v = np.moveaxis(np.asarray(x, np.float32).astype(ml_dtypes.bfloat16).astype(np.float64), axis, -1)
    blocks = v.reshape(v.shape[:-1] + (-1, 32))
    amax = np.abs(blocks).max(-1, keepdims=True)
    byte = np.maximum(np.where(amax > 0, np.frexp(amax)[1] - 1 + 127, 0) - down, 1)
    scale = np.exp2(byte - 127.0)
    codes = (blocks / scale).astype(np.float32).astype(dtype).astype(np.float64)
    return np.moveaxis((codes * scale).reshape(v.shape), -1, axis)


WIDE = False


def mx_kscale(k):
    if not WIDE:
        return np.ones(k)
    levels = np.array([10, -10, 5, -5, 0])
    if k % 512:
        return np.exp2(np.random.permutation(np.resize(levels, k // 32))).repeat(32)
    a = np.empty((k // 512, 16))
    for p in range(k // 512):
        a[p, :8] = np.random.permutation(np.resize(levels, 8))
        for g in range(8):
            far = levels[np.abs(levels - a[p, g]) >= 10]
            a[p, g + 8] = far[np.random.randint(len(far))]
    return np.exp2(a.ravel()).repeat(32)


BF16 = ml_dtypes.bfloat16


def bf(x):
    return np.asarray(x, np.float32).astype(BF16)


def f64(x):
    return np.asarray(x).astype(np.float64)


E2M1 = np.array([0.0, 0.5, 1.0, 1.5, 2.0, 3.0, 4.0, 6.0, -0.0, -0.5, -1.0, -1.5, -2.0, -3.0, -4.0, -6.0])


def pack_weight(w, fmt):
    k, n = w.shape
    w = f64(bf(w)).reshape(k // 32, 32, n)
    amax = np.abs(w).max(1)
    if fmt == "e4m3":
        byte = np.frexp(amax)[1] - 1 + 127 - 7
    else:
        mant, ex = np.frexp(amax / 6.0)
        byte = np.where(mant > 0.5, ex, ex - 1) + 127
    byte = np.clip(np.where(amax > 0, byte, 1), 1, 254)
    scaled = (w * np.exp2(127.0 - byte)[:, None, :]).reshape(k, n).astype(np.float32)
    by_word = np.ascontiguousarray(scaled.reshape(k // 512, 128, 4, n).transpose(0, 1, 3, 2))
    if fmt == "e4m3":
        words = by_word.astype(ml_dtypes.float8_e4m3fn).view(np.uint8)
    else:
        c = by_word.astype(ml_dtypes.float4_e2m1fn).view(np.uint8) & 0xF
        words = c[..., 0::2] | (c[..., 1::2] << 4)
    return np.ascontiguousarray(words), np.ascontiguousarray(byte.astype(np.uint8).reshape(k // 512, 16, n))


def unpack_weight(words, scales, fmt):
    g, p, n, _ = words.shape
    if fmt == "e4m3":
        vals = np.ascontiguousarray(words).view(ml_dtypes.float8_e4m3fn).astype(np.float64)
    else:
        nib = np.empty((g, p, n, 4), np.uint8)
        nib[..., 0::2] = words & 0xF
        nib[..., 1::2] = words >> 4
        vals = E2M1[nib]
    vals = vals * np.repeat(np.exp2(scales.astype(np.float64) - 127.0), 8, axis=1)[..., None]
    return vals.transpose(0, 1, 3, 2).reshape(g * 512, n)
def pack4(w):
    words, scales = pack_weight(w, "e2m1")
    return words.reshape(words.shape[0], 128, -1), scales


def unpack4(words, scales):
    return unpack_weight(words.reshape(words.shape[0], 128, -1, 2), scales, "e2m1")


def planes(Y):
    n, m = Y.shape
    b = f64(bf(Y)).reshape(n // 32, 32, m)
    amax = np.abs(b).max(1)
    byte = np.clip(np.where(amax > 0, np.frexp(amax)[1] - 1 + 127 - 7, 1), 1, 254)
    codes = (b * np.exp2(127.0 - byte)[:, None, :]).reshape(n, m).astype(np.float32).astype(ml_dtypes.float8_e4m3fn).view(np.uint8)
    words = codes.reshape(n // 512, 128, 4, m).transpose(0, 1, 3, 2)
    return np.ascontiguousarray(words), np.ascontiguousarray(byte.astype(np.uint8).reshape(n // 512, 16, m))


M, I, J, D, N = 1536, 64, 32, 512, 1024
K = I * J

def setup_inputs():
    s = mx_kscale(K)
    r = mx_kscale(D)
    u = np.random.randn(M, I) * s.reshape(I, J)[:, 0]
    v = np.random.randn(M, J)
    core = 0.8 * np.random.randn(K, N) / np.sqrt(K) / s[:, None]
    core_words, core_scales = pack4(core)
    x = np.random.randn(M, D) * r
    w = 0.8 * np.random.randn(D, N) / np.sqrt(D) / r[:, None]
    bias = 0.3 * np.random.randn(N)
    gain = np.exp(0.8 * np.random.randn(N))
    return {"u": bf(u), "v": bf(v), "core_words": core_words, "core_scales": core_scales,
            "x": bf(x), "w": bf(w), "bias": bf(bias), "gain": bf(gain)}

def reference(u, v, core_words, core_scales, x, w, bias, gain):
    z = (f64(u)[:, :, None] * f64(v)[:, None, :]).reshape(M, K)
    core = unpack4(core_words, core_scales)
    p = mxq(z, 1, "e4m3") @ core
    q = mxq(f64(x), 1, "e4m3") @ mxq(f64(w), 0, "e4m3")
    y = f64(gain) * np.tanh(p + q + f64(bias))
    Y = y.T
    words, scales = planes(Y)
    return y, words, scales

@@ -1,0 +1,513 @@
+from contextlib import ExitStack
+
+import concourse.mybir as mybir
+from concourse.masks import make_identity
+
+M, I, J, D, N = 1536, 64, 32, 512, 1024
+K = I * J
+FLOPS = 2 * M * (K + D) * N
+
+F32 = mybir.dt.float32
+BF16 = mybir.dt.bfloat16
+I32 = mybir.dt.int32
+U32 = mybir.dt.uint32
+U8 = mybir.dt.uint8
+FP8X4 = mybir.dt.float8_e4m3fn_x4
+FP4X4 = mybir.dt.float4_e2m1fn_x4
+MULT = mybir.AluOpType.mult
+COPY = mybir.ActivationFunctionType.Copy
+TANH = mybir.ActivationFunctionType.Tanh
+
+P = 128
+CH = 512
+NC = M // CH
+G = K // 512
+H = N // 512
+
+
+def tile_neural_tensor_pair_layer_g5_kernel(tc, u, v, core_words, core_scales, x, w, bias, gain, out_0, out_1, out_2):
+    nc = tc.nc
+    with ExitStack() as ctx:
+        sb = ctx.enter_context(tc.tile_pool(name="sb", bufs=1))
+        ps = ctx.enter_context(tc.psum_pool(name="ps", bufs=1))
+
+        def tile(name, shape, dtype):
+            return sb.tile(shape, dtype, name=name, align_bytes=256)
+
+        def tiles(name, count, shape, dtype):
+            return [tile(name + str(k), shape, dtype) for k in range(count)]
+
+        bank = [ps.tile([P, 512], F32, name="bank" + str(k)) for k in range(8)]
+        ident = tile("ident", [P, P], F32)
+        warm = tile("warm", [P, 1], F32)
+        u_raw = tile("u_raw", [P, 12, I], BF16)
+        v_raw = tile("v_raw", [P, 12, J], BF16)
+        u_in = tile("u_in", [P, 2, 2, P], F32)
+        v_in = tile("v_in", [P, 2, P], F32)
+        u_stage = tile("u_stage", [P, 2, 256], F32)
+        v_stage = tile("v_stage", [P, P, 2], F32)
+        core_raw = tile("core_raw", [P, G, 2 * N], U8)
+        core = tile("core", [P, G, 2 * N], U8)
+        cs_raw = tile("cs_raw", [P, 512], U8)
+        cs_perm = tile("cs_perm", [P, 512], U8)
+        u_dup = tile("u_dup", [P, 4, I], F32)
+        u_exp = tile("u_exp", [P, G, 4, P], F32)
+        v_exp = tile("v_exp", [P, 4, 2, P], F32)
+        cs = tile("cs", [P, G, N], U8)
+        w_raw = tiles("w_raw", H, [P, 4, 512], BF16)
+        w_il = tiles("w_il", H, [P, 2048], BF16)
+        w_codes = tiles("w_codes", H, [P, 512], U32)
+        w_sc = tiles("w_sc", H, [P, 512], U8)
+        x_raw = tiles("x_raw", NC, [P, 4, D], BF16)
+        x_split = tile("x_split", [P, 4, 2, P], F32)
+        x_il = tiles("x_il", 2, [P, 2048], BF16)
+        x_codes = tiles("x_codes", NC, [P, CH], U32)
+        x_sc = tiles("x_sc", NC, [P, CH], U8)
+        ub = tiles("ub", 2, [P, G, CH], F32)
+        vb = tiles("vb", 2, [P, 2 * CH], F32)
+        z = tiles("z", 3, [P, 2048], BF16)
+        z_codes = tiles("z_codes", 2, [P, G, CH], U32)
+        z_sc = tiles("z_sc", 2, [P, G, CH], U8)
+        bias_sb = tile("bias_sb", [P, H, 4], BF16)
+        gain_sb = tile("gain_sb", [P, H, 4], BF16)
+        gain32 = tile("gain32", [P, H, 4], F32)
+        y = tiles("y", 4, [P, 4, CH], F32)
+        y_il = tiles("y_il", 2, [P, 2048], BF16)
+        y_codes = tile("y_codes", [P, H, M], U32)
+        y_sc = tile("y_sc", [P, H, M], U8)
+        y_out = tiles("y_out", 2, [P, 4, 512], F32)
+
+        u_park = out_0[M - 80 : M - 16, :].rearrange("r n -> (r n)").rearrange("(c f) -> c f", c=2)
+        v_park = out_0[M - 16 : M, :].rearrange("r n -> (r n)")
+
+        def load_x(c):
+            nc.sync.dma_start(out=x_raw[c][:], in_=x[c * CH : (c + 1) * CH, :].rearrange("(j p) d -> p j d", p=P))
+
+        def load_w(h):
+            nc.sync.dma_start(out=w_raw[h][:], in_=w[:, h * 512 : (h + 1) * 512].rearrange("(p j) n -> p j n", j=4))
+
+        def load_u_raw(t0, t1):
+            nc.sync.dma_start(out=u_raw[:, t0:t1, :], in_=u[t0 * P : t1 * P, :].rearrange("(j p) i -> p j i", p=P))
+
+        def load_core(g0, g1):
+            nc.sync.dma_start(out=core_raw[:, g0:g1, :].bitcast(I32), in_=core_words[g0:g1].rearrange("g p b -> p g b").bitcast(I32))
+
+        def load_ub(c, g0, g1):
+            src = u_park[c - 1].rearrange("(i f) -> i f", i=16)[:, g0 * CH : g1 * CH]
+            nc.sync.dma_start(out=ub[c % 2][:, g0:g1, :].rearrange("p g m -> p (g m)"), in_=src.unsqueeze(1).to_broadcast([16, 8, (g1 - g0) * CH]))
+
+        def load_vb(c):
+            src = v_park[(c - 1) * 8 * 1024 : c * 8 * 1024].rearrange("(j f) -> j f", j=8)
+            nc.sync.dma_start(out=vb[c % 2][:], in_=src.unsqueeze(0).to_broadcast([16, 8, 1024]))
+
+        def load_v_raw(t0, t1):
+            nc.sync.dma_start(out=v_raw[:, t0:t1, :], in_=v[t0 * P : t1 * P, :].rearrange("(j p) i -> p j i", p=P))
+
+        def expand_v():
+            words = v_raw[:, 0:4, :].bitcast(F32).rearrange("p j (q e) -> p j e q", e=2)
+            nc.vector.tensor_copy(
+                out=v_exp[:].rearrange("p j e (r q) -> p j e r q", q=8),
+                in_=words.unsqueeze(3).to_broadcast([P, 4, 2, 16, 8]),
+            )
+
+        def turn_v(b0):
+            for j in range(4):
+                for e in range(2):
+                    col = (2 * (j % 2) + e) * P
+                    nc.tensor.transpose(bank[b0 + j // 2][:, col : col + P], v_exp[:, j, e, :], ident[:])
+
+        def copy_pairs(dst, b0):
+            dst = dst.rearrange("p (j m e) -> p j m e", j=4, e=2)
+            for a in range(2):
+                nc.scalar.copy(out=dst[:, 2 * a : 2 * a + 2], in_=bank[b0 + a][:].rearrange("p (j e m) -> p j m e", j=2, e=2))
+
+        def double_u():
+            nc.vector.tensor_copy(
+                out=u_dup[:].bitcast(BF16).rearrange("p j (i d) -> p j i d", d=2),
+                in_=u_raw[:, 0:4, :].unsqueeze(3).to_broadcast([P, 4, I, 2]),
+            )
+
+        def expand_u(g):
+            nc.vector.tensor_copy(
+                out=u_exp[:, g].rearrange("p j (i r) -> p j i r", r=8),
+                in_=u_dup[:, :, 16 * g : 16 * g + 16].unsqueeze(3).to_broadcast([P, 4, 16, 8]),
+            )
+
+        def turn_u0(g, b):
+            for j in range(4):
+                nc.tensor.transpose(bank[b][:, j * P : (j + 1) * P], u_exp[:, g, j, :], ident[:])
+
+        def order_v():
+            words = v_raw[:, 4:12, :].bitcast(F32).rearrange("p (c j) (q e) -> p e c q j", j=4, e=2)
+            for e in range(2):
+                nc.scalar.copy(out=v_in[:, e, 0:64].rearrange("p (c q j) -> p c q j", c=2, j=4), in_=words[:, e])
+
+        def order_u(c):
+            for jj in range(2):
+                src = u_raw[:, 4 * c + jj : 4 * c + 4 : 2, :].rearrange("p a (g i) -> p i g a", i=16)
+                dst = u_in[:, c - 1, jj, :].bitcast(BF16).rearrange("p (i g a d) -> p i g a d", g=G, a=2, d=2)
+                nc.scalar.copy(out=dst, in_=src.unsqueeze(4).to_broadcast([P, 16, G, 2, 2]))
+
+        def turn_parked(bu, bv):
+            for k in range(4):
+                nc.tensor.transpose(bank[bu][:, k * P : (k + 1) * P], u_in[:, k // 2, k % 2, :], ident[:])
+            for e in range(2):
+                nc.tensor.transpose(bank[bv][:, e * P : (e + 1) * P], v_in[:, e, :], ident[:])
+
+        def park(bu, bv):
+            nc.scalar.copy(out=u_stage[:].rearrange("p c f -> p (c f)"), in_=bank[bu][:])
+            nc.scalar.copy(out=v_stage[0:64], in_=bank[bv][0:64, 0:256].rearrange("p (e m) -> p m e", e=2))
+            nc.sync.dma_start(out=u_park.rearrange("c (p f) -> p c f", p=P), in_=u_stage[:])
+            nc.sync.dma_start(out=v_park.rearrange("(p f) -> p f", p=64), in_=v_stage[0:64].rearrange("p m e -> p (m e)"))
+
+        def permute_core(g, h):
+            cols = slice(h * 1024, (h + 1) * 1024)
+            nc.vector.tensor_copy(
+                out=core[:, g, cols].rearrange("p (t m b) -> p t m b", t=4, b=2),
+                in_=core_raw[:, g, cols].rearrange("p (m t b) -> p t m b", t=4, b=2),
+            )
+
+        def permute_scales():
+            nc.vector.tensor_copy(
+                out=cs_perm[:].rearrange("p (t m) -> p t m", t=4),
+                in_=cs_raw[:].rearrange("p (m t) -> p t m", t=4),
+            )
+            for q in range(4):
+                nc.scalar.dma_start(out=cs[32 * q : 32 * q + 4].bitcast(I32), in_=cs_perm[32 * q : 32 * q + 32, :].bitcast(I32))
+
+        def interleave_w(h):
+            nc.scalar.copy(
+                out=w_il[h][:].rearrange("p (t m j) -> p t m j", t=4, j=4),
+                in_=w_raw[h][:].rearrange("p j (m t) -> p t m j", t=4),
+            )
+
+        def quantize(codes, scales, src):
+            nc.vector.quantize_mx(out=codes.bitcast(FP8X4), scales=scales, in_=src)
+
+        def quant_w(h):
+            quantize(w_codes[h][:], w_sc[h][:], w_il[h][:])
+
+        def split_x(c):
+            nc.scalar.copy(out=x_split[:], in_=x_raw[c][:].bitcast(F32).rearrange("p j (q e) -> p j e q", e=2))
+
+        def turn_x(c, b0):
+            words = x_raw[c][:].bitcast(F32)
+            for j in range(4):
+                for e in range(2):
+                    col = (2 * (j % 2) + e) * P
+                    src = words[:, j, e:256:2] if c == 0 else x_split[:, j, e, :]
+                    nc.tensor.transpose(bank[b0 + j // 2][:, col : col + P], src, ident[:])
+
+        def copy_x(c, b0):
+            copy_pairs(x_il[c % 2][:].bitcast(F32), b0)
+
+        def quant_x(c):
+            quantize(x_codes[c][:], x_sc[c][:], x_il[c % 2][:])
+
+        def mult_z(c, g, b=None, m0=0, m1=CH):
+            src = ub[c % 2][:, g, m0:m1] if b is None else bank[b][:, m0:m1]
+            pair = src.bitcast(BF16).rearrange("p (m d) -> p m d", d=2)
+            nc.vector.tensor_tensor(
+                out=z[(G * c + g) % 3][:, 4 * m0 : 4 * m1].rearrange("p (m a d) -> p m a d", a=2, d=2),
+                in0=vb[c % 2][:, 2 * m0 : 2 * m1].bitcast(BF16).rearrange("p (m a d) -> p m a d", a=2, d=2),
+                in1=pair.unsqueeze(2).to_broadcast([P, m1 - m0, 2, 2]),
+                op=MULT,
+            )
+
+        def quant_z(c, g):
+            quantize(z_codes[c % 2][:, g, :], z_sc[c % 2][:, g, :], z[(G * c + g) % 3][:])
+
+        def mm_core(c, h, t, g, b, start, stop):
+            col = h * 512 + t * P
+            nc.tensor.matmul_mx(
+                out=bank[b][:],
+                lhsT=core[:, g, 2 * col : 2 * col + 2 * P].bitcast(FP4X4),
+                lhsT_scale=cs[:, g, col : col + P],
+                rhs=z_codes[c % 2][:, g, :].bitcast(FP8X4),
+                rhs_scale=z_sc[c % 2][:, g, :],
+                start=start,
+                stop=stop,
+            )
+
+        def mm_x(c, h, t, b, start, stop):
+            nc.tensor.matmul_mx(
+                out=bank[b][:],
+                lhsT=w_codes[h][:, t * P : (t + 1) * P].bitcast(FP8X4),
+                lhsT_scale=w_sc[h][:, t * P : (t + 1) * P],
+                rhs=x_codes[c][:].bitcast(FP8X4),
+                rhs_scale=x_sc[c][:],
+                start=start,
+                stop=stop,
+            )
+
+        def quarter_group(n, t, j, b):
+            c, h = divmod(n, H)
+            col = h * 512 + t * P
+            tok = slice(j * P, (j + 1) * P)
+            nc.tensor.matmul_mx(out=bank[b][:, tok], lhsT=w_codes[h][:, t * P : (t + 1) * P].bitcast(FP8X4), lhsT_scale=w_sc[h][:, t * P : (t + 1) * P],
+                                rhs=x_codes[c][:, tok].bitcast(FP8X4), rhs_scale=x_sc[c][:, tok], start=True, stop=False)
+            for g in range(G):
+                nc.tensor.matmul_mx(out=bank[b][:, tok], lhsT=core[:, g, 2 * col : 2 * col + 2 * P].bitcast(FP4X4), lhsT_scale=cs[:, g, col : col + P],
+                                    rhs=z_codes[c % 2][:, g, tok].bitcast(FP8X4), rhs_scale=z_sc[c % 2][:, g, tok], start=False, stop=g == G - 1)
+
+        def group(n, t):
+            c, h = divmod(n, H)
+            mm_x(c, h, t, t, True, False)
+            for g in range(G):
+                mm_core(c, h, t, g, t, False, g == G - 1)
+
+        def tanh(n, t, b, m0=0, m1=CH):
+            nc.scalar.activation(out=y[n % 4][:, t, m0:m1], in_=bank[b][:, m0:m1], func=TANH, bias=bias_sb[:, n % H, t : t + 1])
+
+        def scale_s(n, t):
+            nc.scalar.activation(out=y[n % 4][:, t, :], in_=y[n % 4][:, t, :], func=COPY, scale=gain32[:, n % H, t : t + 1])
+
+        def scale(n, t, m0=0, m1=CH):
+            nc.vector.tensor_scalar(out=y[n % 4][:, t, m0:m1], in0=y[n % 4][:, t, m0:m1], scalar1=gain_sb[:, n % H, t : t + 1], scalar2=None, op0=MULT)
+
+        def interleave_y(n, m0=0, m1=CH):
+            nc.vector.tensor_copy(
+                out=y_il[n % 2][:, 4 * m0 : 4 * m1].rearrange("p (c i t) -> p c t i", i=4, t=4),
+                in_=y[n % 4][:, :, m0:m1].rearrange("p t (c i) -> p c t i", i=4),
+            )
+
+        def quant_y(n, m0=0, m1=CH):
+            c, h = divmod(n, H)
+            cols = slice(c * CH + m0, c * CH + m1)
+            quantize(y_codes[:, h, cols], y_sc[:, h, cols], y_il[n % 2][:, 4 * m0 : 4 * m1])
+
+        def store_words(n):
+            c, h = divmod(n, H)
+            cols = slice(c * CH, (c + 1) * CH)
+            nc.sync.dma_start(out=out_1[h, :, cols, :].rearrange("p m t -> p (m t)").bitcast(I32), in_=y_codes[:, h, cols].bitcast(I32))
+
+        def store_scales(c0, c1):
+            cols = slice(c0 * CH, c1 * CH)
+            for q in range(4):
+                nc.sync.dma_start(
+                    out=out_2[:, 4 * q : 4 * q + 4, cols].rearrange("h r m -> r h m").bitcast(I32),
+                    in_=y_sc[32 * q : 32 * q + 4, :, cols].bitcast(I32),
+                )
+
+        def turn_y(n, ts, js=range(4)):
+            for t in ts:
+                for j in js:
+                    nc.tensor.transpose(bank[4 + j][:, t * P : (t + 1) * P], y[n % 4][:, t, j * P : (j + 1) * P], ident[:])
+
+        def copy_y(n, j, engine):
+            dst = y_out[n % 2][:, j, :].rearrange("m (p t) -> m p t", t=4)
+            src = bank[4 + j][:].rearrange("m (t p) -> m p t", t=4)
+            if engine == "vector":
+                nc.vector.tensor_copy(out=dst, in_=src)
+            else:
+                nc.scalar.copy(out=dst, in_=src)
+
+        def store_y(n, j0, j1):
+            c, h = divmod(n, H)
+            rows = out_0[c * CH + j0 * P : c * CH + j1 * P, h * 512 : (h + 1) * 512]
+            nc.sync.dma_start(out=rows.rearrange("(j m) n -> m j n", m=P), in_=y_out[n % 2][:, j0:j1, :])
+
+        with tc.manual_schedule():
+            nc.vector.memset(v_in[:, :, 64:P], 0.0)
+            make_identity(nc, ident[:])
+            nc.gpsimd.memset(cs[:].rearrange("p g n -> p (g n)").bitcast(I32), 0)
+            nc.scalar.activation(out=warm[:], in_=v_in[:, 0, 64:65], func=TANH)
+            for k in range(16):
+                nc.tensor.transpose(bank[7][:, 0:P], ident[:], ident[:])
+            load_v_raw(0, 4)
+            for h in range(H):
+                nc.sync.dma_start(out=cs_raw[h:P:2, :].bitcast(I32), in_=core_scales[:, :, h * 512 : (h + 1) * 512].rearrange("g q n -> q g n").bitcast(I32))
+            load_u_raw(0, 4)
+            load_core(0, 1)
+            load_u_raw(4, 12)
+            load_v_raw(4, 12)
+            load_x(0)
+            load_core(1, 2)
+            expand_v()
+            permute_scales()
+            double_u()
+            turn_v(0)
+            copy_pairs(vb[0][:], 0)
+            load_w(0)
+            load_core(2, G)
+            load_w(1)
+            permute_core(0, 0)
+            expand_u(0)
+            expand_u(1)
+            turn_u0(0, 6)
+            turn_u0(1, 7)
+            order_v()
+            order_u(1)
+            order_u(2)
+            expand_u(2)
+            expand_u(3)
+            mult_z(0, 0, 6)
+            turn_u0(2, 0)
+            turn_u0(3, 1)
+            for g in range(2, G):
+                nc.scalar.copy(out=ub[0][:, g, :], in_=bank[g - 2][:])
+            turn_parked(2, 3)
+            park(2, 3)
+            turn_x(0, 4)
+            copy_x(0, 4)
+            nc.sync.dma_start(out=bias_sb[:], in_=bias.rearrange("(h p t) -> p h t", h=H, t=4))
+            nc.sync.dma_start(out=gain_sb[:], in_=gain.rearrange("(h p t) -> p h t", h=H, t=4))
+            load_x(1)
+            load_vb(1)
+            load_ub(1, 0, G)
+            load_x(2)
+            interleave_w(0)
+            interleave_w(1)
+            split_x(1)
+            permute_core(0, 1)
+            quant_z(0, 0)
+            mult_z(0, 1, 7)
+            permute_core(1, 0)
+            quant_z(0, 1)
+            permute_core(1, 1)
+            mult_z(0, 2)
+            permute_core(2, 0)
+            quant_z(0, 2)
+            permute_core(2, 1)
+            quant_x(0)
+            quant_w(0)
+            mult_z(0, 3)
+            permute_core(3, 0)
+            quant_z(0, 3)
+            quant_w(1)
+            permute_core(3, 1)
+            nc.scalar.copy(out=gain32[:], in_=gain_sb[:])
+            for g in range(3):
+                for b in range(8):
+                    mm_core(0, b // 4, b % 4, g, b, g == 0, False)
+            for t in range(4):
+                mm_x(0, 0, t, t, False, False)
+            for t in range(4):
+                mm_core(0, 0, t, 3, t, False, True)
+                tanh(0, t, t)
+            for t in range(4):
+                mm_x(0, 1, t, 4 + t, False, False)
+            load_vb(2)
+            load_ub(2, 0, G)
+            mult_z(1, 0)
+            mult_z(1, 1)
+            quant_z(1, 0)
+            mult_z(1, 2)
+            quant_z(1, 1)
+            for t in range(4):
+                mm_core(0, 1, t, 3, 4 + t, False, True)
+                tanh(1, t, 4 + t)
+            mult_z(1, 3)
+            quant_z(1, 2)
+            for t in range(4):
+                mm_core(1, 0, t, 0, t, True, False)
+            turn_x(1, 4)
+            copy_x(1, 4)
+            for t in range(4):
+                scale_s(0, t)
+            split_x(2)
+            quant_z(1, 3)
+            quant_x(1)
+            for g in range(1, G):
+                for t in range(4):
+                    mm_core(1, 0, t, g, t, False, False)
+            for t in range(4):
+                mm_x(1, 0, t, t, False, True)
+                tanh(2, t, t)
+            turn_y(0, range(4))
+            for t in range(4):
+                scale(1, t)
+            mult_z(2, 0)
+            interleave_y(0)
+            quant_z(2, 0)
+            quant_y(0)
+            for j in range(4):
+                copy_y(0, j, "scalar")
+            store_y(0, 0, 4)
+            store_words(0)
+            for t in range(2):
+                group(3, t)
+                tanh(3, t, t)
+            turn_x(2, 2)
+            copy_x(2, 2)
+            turn_y(1, range(4))
+            mult_z(2, 1)
+            for t in range(4):
+                scale(2, t)
+            quant_z(2, 1)
+            mult_z(2, 2)
+            quant_x(2)
+            quant_z(2, 2)
+            mult_z(2, 3)
+            scale(3, 0)
+            scale(3, 1)
+            quant_z(2, 3)
+            for j in range(4):
+                copy_y(1, j, "scalar")
+            store_y(1, 0, 4)
+            for t in range(2, 4):
+                group(3, t)
+                tanh(3, t, t)
+            turn_y(2, range(4))
+            interleave_y(1)
+            scale(3, 2)
+            quant_y(1)
+            scale(3, 3)
+            store_words(1)
+            for j in range(4):
+                copy_y(2, j, "scalar")
+            store_y(2, 0, 4)
+            for t in range(2):
+                group(4, t)
+                tanh(4, t, t)
+            turn_y(3, range(4))
+            for j in range(4):
+                copy_y(3, j, "scalar")
+            store_y(3, 0, 4)
+            interleave_y(2)
+            interleave_y(3)
+            quant_y(2)
+            quant_y(3)
+            store_words(2)
+            store_words(3)
+            store_scales(0, 2)
+            for t in range(2, 4):
+                group(4, t)
+                tanh(4, t, t)
+            for t in range(4):
+                scale(4, t)
+            group(5, 0)
+            tanh(5, 0, 0)
+            interleave_y(4)
+            turn_y(4, range(4))
+            scale(5, 0)
+            quant_y(4)
+            for j in range(4):
+                copy_y(4, j, "scalar" if j % 2 else "vector")
+            store_words(4)
+            store_y(4, 0, 4)
+            for t in range(1, 3):
+                group(5, t)
+                tanh(5, t, t)
+                scale(5, t)
+            for j in range(4):
+                b = (0, 1, 3, 2)[j]
+                quarter_group(5, 3, j, b)
+                tanh(5, 3, b, j * P, j * P + P)
+                scale(5, 3, j * P, j * P + P)
+                if j == 1:
+                    interleave_y(5, 0, 256)
+                if j == 2:
+                    quant_y(5, 0, 256)
+            for j in range(4):
+                turn_y(5, range(4), [j])
+            interleave_y(5, 256, 512)
+            quant_y(5, 256, 512)
+            for j in range(2):
+                copy_y(5, j, "scalar")
+                store_y(5, j, j + 1)
+            store_words(5)
+            store_scales(2, 3)
+            copy_y(5, 2, "scalar")
+            copy_y(5, 3, "vector")
+            store_y(5, 2, 4)

@@ -195,7 +195,7 @@ def tile_neural_tensor_pair_layer_g5_kernel(tc, u, v, core_words, core_scales, x
             for j in range(4):
                 for e in range(2):
                     col = (2 * (j % 2) + e) * P
-                    src = words[:, j, e:256:2] if c == 0 else x_split[:, j, e, :]
+                    src = words[:, j, e:256:2]
                     nc.tensor.transpose(bank[b0 + j // 2][:, col : col + P], src, ident[:])
 
         def copy_x(c, b0):
@@ -267,8 +267,8 @@ def tile_neural_tensor_pair_layer_g5_kernel(tc, u, v, core_words, core_scales, x
 
         def interleave_y(n, m0=0, m1=CH):
             nc.vector.tensor_copy(
-                out=y_il[n % 2][:, 4 * m0 : 4 * m1].rearrange("p (c i t) -> p c t i", i=4, t=4),
-                in_=y[n % 4][:, :, m0:m1].rearrange("p t (c i) -> p c t i", i=4),
+                out=y_il[n % 2][:, 4 * m0 : 4 * m1].rearrange("p (m t) -> p m t", t=4),
+                in_=y[n % 4][:, :, m0:m1].rearrange("p t m -> p m t"),
             )
 
         def quant_y(n, m0=0, m1=CH):
@@ -309,8 +309,8 @@ def tile_neural_tensor_pair_layer_g5_kernel(tc, u, v, core_words, core_scales, x
 
         with tc.manual_schedule():
             nc.vector.memset(v_in[:, :, 64:P], 0.0)
+            nc.vector.memset(cs[:].rearrange("p g n -> p (g n)").bitcast(I32), 0)
             make_identity(nc, ident[:])
-            nc.gpsimd.memset(cs[:].rearrange("p g n -> p (g n)").bitcast(I32), 0)
             nc.scalar.activation(out=warm[:], in_=v_in[:, 0, 64:65], func=TANH)
             for k in range(16):
                 nc.tensor.transpose(bank[7][:, 0:P], ident[:], ident[:])
@@ -319,46 +319,46 @@ def tile_neural_tensor_pair_layer_g5_kernel(tc, u, v, core_words, core_scales, x
                 nc.sync.dma_start(out=cs_raw[h:P:2, :].bitcast(I32), in_=core_scales[:, :, h * 512 : (h + 1) * 512].rearrange("g q n -> q g n").bitcast(I32))
             load_u_raw(0, 4)
             load_core(0, 1)
-            load_u_raw(4, 12)
             load_v_raw(4, 12)
+            load_u_raw(4, 12)
             load_x(0)
             load_core(1, 2)
             expand_v()
             permute_scales()
             double_u()
-            turn_v(0)
-            copy_pairs(vb[0][:], 0)
+            turn_v(5)
+            copy_pairs(vb[0][:], 5)
             load_w(0)
             load_core(2, G)
-            load_w(1)
             permute_core(0, 0)
             expand_u(0)
             expand_u(1)
-            turn_u0(0, 6)
+            turn_u0(0, 0)
             turn_u0(1, 7)
             order_v()
             order_u(1)
             order_u(2)
             expand_u(2)
             expand_u(3)
-            mult_z(0, 0, 6)
-            turn_u0(2, 0)
-            turn_u0(3, 1)
+            mult_z(0, 0, 0)
+            turn_u0(2, 3)
+            turn_u0(3, 4)
+            turn_parked(1, 2)
+            park(1, 2)
             for g in range(2, G):
-                nc.scalar.copy(out=ub[0][:, g, :], in_=bank[g - 2][:])
-            turn_parked(2, 3)
-            park(2, 3)
-            turn_x(0, 4)
-            copy_x(0, 4)
+                nc.scalar.copy(out=ub[0][:, g, :], in_=bank[g + 1][:])
+            turn_x(0, 5)
+            copy_x(0, 5)
+            load_w(1)
+            load_vb(1)
+            load_ub(1, 0, 1)
             nc.sync.dma_start(out=bias_sb[:], in_=bias.rearrange("(h p t) -> p h t", h=H, t=4))
             nc.sync.dma_start(out=gain_sb[:], in_=gain.rearrange("(h p t) -> p h t", h=H, t=4))
+            load_ub(1, 1, G)
             load_x(1)
-            load_vb(1)
-            load_ub(1, 0, G)
             load_x(2)
             interleave_w(0)
             interleave_w(1)
-            split_x(1)
             permute_core(0, 1)
             quant_z(0, 0)
             mult_z(0, 1, 7)
@@ -405,7 +405,6 @@ def tile_neural_tensor_pair_layer_g5_kernel(tc, u, v, core_words, core_scales, x
             copy_x(1, 4)
             for t in range(4):
                 scale_s(0, t)
-            split_x(2)
             quant_z(1, 3)
             quant_x(1)
             for g in range(1, G):
@@ -418,30 +417,29 @@ def tile_neural_tensor_pair_layer_g5_kernel(tc, u, v, core_words, core_scales, x
             for t in range(4):
                 scale(1, t)
             mult_z(2, 0)
-            interleave_y(0)
+            mult_z(2, 1)
             quant_z(2, 0)
-            quant_y(0)
+            mult_z(2, 2)
+            quant_z(2, 1)
+            mult_z(2, 3)
+            quant_z(2, 2)
             for j in range(4):
                 copy_y(0, j, "scalar")
             store_y(0, 0, 4)
-            store_words(0)
             for t in range(2):
                 group(3, t)
                 tanh(3, t, t)
             turn_x(2, 2)
             copy_x(2, 2)
             turn_y(1, range(4))
-            mult_z(2, 1)
-            for t in range(4):
-                scale(2, t)
-            quant_z(2, 1)
-            mult_z(2, 2)
-            quant_x(2)
-            quant_z(2, 2)
-            mult_z(2, 3)
-            scale(3, 0)
-            scale(3, 1)
+            scale(2, 0)
             quant_z(2, 3)
+            for t in range(1, 4):
+                scale(2, t)
+            interleave_y(0)
+            quant_x(2)
+            quant_y(0)
+            store_words(0)
             for j in range(4):
                 copy_y(1, j, "scalar")
             store_y(1, 0, 4)
@@ -450,7 +448,8 @@ def tile_neural_tensor_pair_layer_g5_kernel(tc, u, v, core_words, core_scales, x
                 tanh(3, t, t)
             turn_y(2, range(4))
             interleave_y(1)
-            scale(3, 2)
+            for t in range(3):
+                scale(3, t)
             quant_y(1)
             scale(3, 3)
             store_words(1)
@@ -494,20 +493,20 @@ def tile_neural_tensor_pair_layer_g5_kernel(tc, u, v, core_words, core_scales, x
                 b = (0, 1, 3, 2)[j]
                 quarter_group(5, 3, j, b)
                 tanh(5, 3, b, j * P, j * P + P)
-                scale(5, 3, j * P, j * P + P)
-                if j == 1:
+                if j == 3:
                     interleave_y(5, 0, 256)
-                if j == 2:
-                    quant_y(5, 0, 256)
+                scale(5, 3, j * P, j * P + P)
             for j in range(4):
                 turn_y(5, range(4), [j])
+            quant_y(5, 0, 256)
             interleave_y(5, 256, 512)
+            copy_y(5, 0, "scalar")
+            store_y(5, 0, 1)
+            copy_y(5, 1, "vector")
+            copy_y(5, 2, "scalar")
+            store_y(5, 1, 3)
             quant_y(5, 256, 512)
-            for j in range(2):
-                copy_y(5, j, "scalar")
-                store_y(5, j, j + 1)
             store_words(5)
             store_scales(2, 3)
-            copy_y(5, 2, "scalar")
-            copy_y(5, 3, "vector")
-            store_y(5, 2, 4)
+            copy_y(5, 3, "scalar")
+            store_y(5, 3, 4)

@@ -40,6 +40,9 @@ def tile_neural_tensor_pair_layer_g5_kernel(tc, u, v, core_words, core_scales, x
         bank = [ps.tile([P, 512], F32, name="bank" + str(k)) for k in range(8)]
         ident = tile("ident", [P, P], F32)
         warm = tile("warm", [P, 1], F32)
+        idle_in = tile("idle_in", [P, 1024], BF16)
+        idle_codes = tile("idle_codes", [P, 256], U32)
+        idle_sc = tile("idle_sc", [P, 256], U8)
         u_raw = tile("u_raw", [P, 12, I], BF16)
         v_raw = tile("v_raw", [P, 12, J], BF16)
         u_in = tile("u_in", [P, 2, 2, P], F32)
@@ -59,7 +62,6 @@ def tile_neural_tensor_pair_layer_g5_kernel(tc, u, v, core_words, core_scales, x
         w_codes = tiles("w_codes", H, [P, 512], U32)
         w_sc = tiles("w_sc", H, [P, 512], U8)
         x_raw = tiles("x_raw", NC, [P, 4, D], BF16)
-        x_split = tile("x_split", [P, 4, 2, P], F32)
         x_il = tiles("x_il", 2, [P, 2048], BF16)
         x_codes = tiles("x_codes", NC, [P, CH], U32)
         x_sc = tiles("x_sc", NC, [P, CH], U8)
@@ -187,9 +189,6 @@ def tile_neural_tensor_pair_layer_g5_kernel(tc, u, v, core_words, core_scales, x
         def quant_w(h):
             quantize(w_codes[h][:], w_sc[h][:], w_il[h][:])
 
-        def split_x(c):
-            nc.scalar.copy(out=x_split[:], in_=x_raw[c][:].bitcast(F32).rearrange("p j (q e) -> p j e q", e=2))
-
         def turn_x(c, b0):
             words = x_raw[c][:].bitcast(F32)
             for j in range(4):
@@ -239,6 +238,11 @@ def tile_neural_tensor_pair_layer_g5_kernel(tc, u, v, core_words, core_scales, x
                 start=start,
                 stop=stop,
             )
+
+        def keep_warm(count, b):
+            for k in range(count):
+                nc.tensor.matmul_mx(out=bank[b][:, 0:256], lhsT=idle_codes[:, 0:P].bitcast(FP8X4), lhsT_scale=idle_sc[:, 0:P],
+                                    rhs=idle_codes[:].bitcast(FP8X4), rhs_scale=idle_sc[:], start=True, stop=True)
 
         def quarter_group(n, t, j, b):
             c, h = divmod(n, H)
@@ -290,8 +294,8 @@ def tile_neural_tensor_pair_layer_g5_kernel(tc, u, v, core_words, core_scales, x
                 )
 
         def turn_y(n, ts, js=range(4)):
-            for t in ts:
-                for j in js:
+            for j in js:
+                for t in ts:
                     nc.tensor.transpose(bank[4 + j][:, t * P : (t + 1) * P], y[n % 4][:, t, j * P : (j + 1) * P], ident[:])
 
         def copy_y(n, j, engine):
@@ -308,12 +312,13 @@ def tile_neural_tensor_pair_layer_g5_kernel(tc, u, v, core_words, core_scales, x
             nc.sync.dma_start(out=rows.rearrange("(j m) n -> m j n", m=P), in_=y_out[n % 2][:, j0:j1, :])
 
         with tc.manual_schedule():
+            nc.vector.memset(idle_in[:].bitcast(I32), 0)
             nc.vector.memset(v_in[:, :, 64:P], 0.0)
+            quantize(idle_codes[:], idle_sc[:], idle_in[:])
             nc.vector.memset(cs[:].rearrange("p g n -> p (g n)").bitcast(I32), 0)
             make_identity(nc, ident[:])
             nc.scalar.activation(out=warm[:], in_=v_in[:, 0, 64:65], func=TANH)
-            for k in range(16):
-                nc.tensor.transpose(bank[7][:, 0:P], ident[:], ident[:])
+            keep_warm(7, 7)
             load_v_raw(0, 4)
             for h in range(H):
                 nc.sync.dma_start(out=cs_raw[h:P:2, :].bitcast(I32), in_=core_scales[:, :, h * 512 : (h + 1) * 512].rearrange("g q n -> q g n").bitcast(I32))
@@ -328,6 +333,7 @@ def tile_neural_tensor_pair_layer_g5_kernel(tc, u, v, core_words, core_scales, x
             double_u()
             turn_v(5)
             copy_pairs(vb[0][:], 5)
+            keep_warm(5, 1)
             load_w(0)
             load_core(2, G)
             permute_core(0, 0)
@@ -343,10 +349,11 @@ def tile_neural_tensor_pair_layer_g5_kernel(tc, u, v, core_words, core_scales, x
             mult_z(0, 0, 0)
             turn_u0(2, 3)
             turn_u0(3, 4)
+            keep_warm(3, 1)
             turn_parked(1, 2)
-            park(1, 2)
             for g in range(2, G):
                 nc.scalar.copy(out=ub[0][:, g, :], in_=bank[g + 1][:])
+            park(1, 2)
             turn_x(0, 5)
             copy_x(0, 5)
             load_w(1)
@@ -375,7 +382,9 @@ def tile_neural_tensor_pair_layer_g5_kernel(tc, u, v, core_words, core_scales, x
             permute_core(3, 0)
             quant_z(0, 3)
             quant_w(1)
+            mult_z(1, 0)
             permute_core(3, 1)
+            quant_z(1, 0)
             nc.scalar.copy(out=gain32[:], in_=gain_sb[:])
             for g in range(3):
                 for b in range(8):
@@ -389,9 +398,7 @@ def tile_neural_tensor_pair_layer_g5_kernel(tc, u, v, core_words, core_scales, x
                 mm_x(0, 1, t, 4 + t, False, False)
             load_vb(2)
             load_ub(2, 0, G)
-            mult_z(1, 0)
             mult_z(1, 1)
-            quant_z(1, 0)
             mult_z(1, 2)
             quant_z(1, 1)
             for t in range(4):
@@ -485,28 +492,28 @@ def tile_neural_tensor_pair_layer_g5_kernel(tc, u, v, core_words, core_scales, x
                 copy_y(4, j, "scalar" if j % 2 else "vector")
             store_words(4)
             store_y(4, 0, 4)
-            for t in range(1, 3):
-                group(5, t)
-                tanh(5, t, t)
-                scale(5, t)
+            group(5, 1)
+            tanh(5, 1, 1)
+            scale(5, 1)
             for j in range(4):
-                b = (0, 1, 3, 2)[j]
-                quarter_group(5, 3, j, b)
-                tanh(5, 3, b, j * P, j * P + P)
-                if j == 3:
+                for t in range(2, 4):
+                    b = (2, 3, 0, 1)[2 * (j % 2) + t - 2]
+                    quarter_group(5, t, j, b)
+                    tanh(5, t, b, j * P, j * P + P)
+                    scale(5, t, j * P, j * P + P)
+                if j == 2:
+                    turn_y(5, range(4), [0, 1])
                     interleave_y(5, 0, 256)
-                scale(5, 3, j * P, j * P + P)
-            for j in range(4):
-                turn_y(5, range(4), [j])
+                    copy_y(5, 0, "scalar")
+                    copy_y(5, 1, "vector")
+                    store_y(5, 0, 2)
+            turn_y(5, range(4), [2, 3])
             quant_y(5, 0, 256)
             interleave_y(5, 256, 512)
-            copy_y(5, 0, "scalar")
-            store_y(5, 0, 1)
-            copy_y(5, 1, "vector")
             copy_y(5, 2, "scalar")
-            store_y(5, 1, 3)
+            store_y(5, 2, 3)
             quant_y(5, 256, 512)
-            store_words(5)
-            store_scales(2, 3)
             copy_y(5, 3, "scalar")
             store_y(5, 3, 4)
+            store_words(5)
+            store_scales(2, 3)

@@ -54,10 +54,7 @@ def tile_neural_tensor_pair_layer_g5_kernel(tc, u, v, core_words, core_scales, x
         cs_raw = tile("cs_raw", [P, 512], U8)
         cs_perm = tile("cs_perm", [P, 512], U8)
         u_dup = tile("u_dup", [P, 4, I], F32)
-        u_exp = tile("u_exp", [P, G, 4, P], F32)
-        v_exp = tile("v_exp", [P, 4, 2, P], F32)
         cs = tile("cs", [P, G, N], U8)
-        w_raw = tiles("w_raw", H, [P, 4, 512], BF16)
         w_il = tiles("w_il", H, [P, 2048], BF16)
         w_codes = tiles("w_codes", H, [P, 512], U32)
         w_sc = tiles("w_sc", H, [P, 512], U8)
@@ -73,11 +70,14 @@ def tile_neural_tensor_pair_layer_g5_kernel(tc, u, v, core_words, core_scales, x
         bias_sb = tile("bias_sb", [P, H, 4], BF16)
         gain_sb = tile("gain_sb", [P, H, 4], BF16)
         gain32 = tile("gain32", [P, H, 4], F32)
-        y = tiles("y", 4, [P, 4, CH], F32)
+        y = tiles("y", 6, [P, 4, CH], F32)
         y_il = tiles("y_il", 2, [P, 2048], BF16)
         y_codes = tile("y_codes", [P, H, M], U32)
         y_sc = tile("y_sc", [P, H, M], U8)
         y_out = tiles("y_out", 2, [P, 4, 512], F32)
+        u_exp = y_out[1][:].rearrange("p g (j c) -> p g j c", j=4)
+        v_exp = y_out[0][:, 0:2, :].rearrange("p a (b e c) -> p (a b) e c", e=2, c=P)
+        w_raw = [y[5][:, 2 * h : 2 * h + 2, :].rearrange("p a c -> p (a c)").bitcast(BF16).rearrange("p (j n) -> p j n", j=4) for h in range(H)]
 
         u_park = out_0[M - 80 : M - 16, :].rearrange("r n -> (r n)").rearrange("(c f) -> c f", c=2)
         v_park = out_0[M - 16 : M, :].rearrange("r n -> (r n)")
@@ -150,17 +150,21 @@ def tile_neural_tensor_pair_layer_g5_kernel(tc, u, v, core_words, core_scales, x
                 dst = u_in[:, c - 1, jj, :].bitcast(BF16).rearrange("p (i g a d) -> p i g a d", g=G, a=2, d=2)
                 nc.scalar.copy(out=dst, in_=src.unsqueeze(4).to_broadcast([P, 16, G, 2, 2]))
 
-        def turn_parked(bu, bv):
-            for k in range(4):
-                nc.tensor.transpose(bank[bu][:, k * P : (k + 1) * P], u_in[:, k // 2, k % 2, :], ident[:])
+        def turn_parked_v(b):
             for e in range(2):
-                nc.tensor.transpose(bank[bv][:, e * P : (e + 1) * P], v_in[:, e, :], ident[:])
+                nc.tensor.transpose(bank[b][:, e * P : (e + 1) * P], v_in[:, e, :], ident[:])
 
-        def park(bu, bv):
-            nc.scalar.copy(out=u_stage[:].rearrange("p c f -> p (c f)"), in_=bank[bu][:])
-            nc.scalar.copy(out=v_stage[0:64], in_=bank[bv][0:64, 0:256].rearrange("p (e m) -> p m e", e=2))
-            nc.sync.dma_start(out=u_park.rearrange("c (p f) -> p c f", p=P), in_=u_stage[:])
+        def park_v(b):
+            nc.scalar.copy(out=v_stage[0:64], in_=bank[b][0:64, 0:256].rearrange("p (e m) -> p m e", e=2))
             nc.sync.dma_start(out=v_park.rearrange("(p f) -> p f", p=64), in_=v_stage[0:64].rearrange("p m e -> p (m e)"))
+
+        def turn_parked_u(b):
+            for k in range(4):
+                nc.tensor.transpose(bank[b][:, k * P : (k + 1) * P], u_in[:, k // 2, k % 2, :], ident[:])
+
+        def park_u(b):
+            nc.scalar.copy(out=u_stage[:].rearrange("p c f -> p (c f)"), in_=bank[b][:])
+            nc.sync.dma_start(out=u_park.rearrange("c (p f) -> p c f", p=P), in_=u_stage[:])
 
         def permute_core(g, h):
             cols = slice(h * 1024, (h + 1) * 1024)
@@ -261,18 +265,18 @@ def tile_neural_tensor_pair_layer_g5_kernel(tc, u, v, core_words, core_scales, x
                 mm_core(c, h, t, g, t, False, g == G - 1)
 
         def tanh(n, t, b, m0=0, m1=CH):
-            nc.scalar.activation(out=y[n % 4][:, t, m0:m1], in_=bank[b][:, m0:m1], func=TANH, bias=bias_sb[:, n % H, t : t + 1])
+            nc.scalar.activation(out=y[n][:, t, m0:m1], in_=bank[b][:, m0:m1], func=TANH, bias=bias_sb[:, n % H, t : t + 1])
 
         def scale_s(n, t):
-            nc.scalar.activation(out=y[n % 4][:, t, :], in_=y[n % 4][:, t, :], func=COPY, scale=gain32[:, n % H, t : t + 1])
+            nc.scalar.activation(out=y[n][:, t, :], in_=y[n][:, t, :], func=COPY, scale=gain32[:, n % H, t : t + 1])
 
         def scale(n, t, m0=0, m1=CH):
-            nc.vector.tensor_scalar(out=y[n % 4][:, t, m0:m1], in0=y[n % 4][:, t, m0:m1], scalar1=gain_sb[:, n % H, t : t + 1], scalar2=None, op0=MULT)
+            nc.vector.tensor_scalar(out=y[n][:, t, m0:m1], in0=y[n][:, t, m0:m1], scalar1=gain_sb[:, n % H, t : t + 1], scalar2=None, op0=MULT)
 
         def interleave_y(n, m0=0, m1=CH):
             nc.vector.tensor_copy(
                 out=y_il[n % 2][:, 4 * m0 : 4 * m1].rearrange("p (m t) -> p m t", t=4),
-                in_=y[n % 4][:, :, m0:m1].rearrange("p t m -> p m t"),
+                in_=y[n][:, :, m0:m1].rearrange("p t m -> p m t"),
             )
 
         def quant_y(n, m0=0, m1=CH):
@@ -296,7 +300,7 @@ def tile_neural_tensor_pair_layer_g5_kernel(tc, u, v, core_words, core_scales, x
         def turn_y(n, ts, js=range(4)):
             for j in js:
                 for t in ts:
-                    nc.tensor.transpose(bank[4 + j][:, t * P : (t + 1) * P], y[n % 4][:, t, j * P : (j + 1) * P], ident[:])
+                    nc.tensor.transpose(bank[4 + j][:, t * P : (t + 1) * P], y[n][:, t, j * P : (j + 1) * P], ident[:])
 
         def copy_y(n, j, engine):
             dst = y_out[n % 2][:, j, :].rearrange("m (p t) -> m p t", t=4)
@@ -320,54 +324,55 @@ def tile_neural_tensor_pair_layer_g5_kernel(tc, u, v, core_words, core_scales, x
             nc.scalar.activation(out=warm[:], in_=v_in[:, 0, 64:65], func=TANH)
             keep_warm(7, 7)
             load_v_raw(0, 4)
+            load_u_raw(0, 4)
             for h in range(H):
                 nc.sync.dma_start(out=cs_raw[h:P:2, :].bitcast(I32), in_=core_scales[:, :, h * 512 : (h + 1) * 512].rearrange("g q n -> q g n").bitcast(I32))
-            load_u_raw(0, 4)
             load_core(0, 1)
             load_v_raw(4, 12)
             load_u_raw(4, 12)
             load_x(0)
             load_core(1, 2)
             expand_v()
-            permute_scales()
             double_u()
+            permute_scales()
             turn_v(5)
             copy_pairs(vb[0][:], 5)
-            keep_warm(5, 1)
+            keep_warm(5, 3)
             load_w(0)
-            load_core(2, G)
+            load_core(2, 3)
             permute_core(0, 0)
-            expand_u(0)
-            expand_u(1)
+            for g in range(G):
+                expand_u(g)
             turn_u0(0, 0)
             turn_u0(1, 7)
             order_v()
             order_u(1)
             order_u(2)
-            expand_u(2)
-            expand_u(3)
+            turn_u0(2, 1)
+            turn_u0(3, 2)
+            turn_parked_v(3)
+            turn_parked_u(4)
             mult_z(0, 0, 0)
-            turn_u0(2, 3)
-            turn_u0(3, 4)
-            keep_warm(3, 1)
-            turn_parked(1, 2)
-            for g in range(2, G):
-                nc.scalar.copy(out=ub[0][:, g, :], in_=bank[g + 1][:])
-            park(1, 2)
-            turn_x(0, 5)
-            copy_x(0, 5)
-            load_w(1)
-            load_vb(1)
-            load_ub(1, 0, 1)
-            nc.sync.dma_start(out=bias_sb[:], in_=bias.rearrange("(h p t) -> p h t", h=H, t=4))
-            nc.sync.dma_start(out=gain_sb[:], in_=gain.rearrange("(h p t) -> p h t", h=H, t=4))
-            load_ub(1, 1, G)
-            load_x(1)
-            load_x(2)
-            interleave_w(0)
-            interleave_w(1)
             permute_core(0, 1)
             quant_z(0, 0)
+            for g in range(2, G):
+                nc.scalar.copy(out=ub[0][:, g, :], in_=bank[g - 1][:])
+            load_w(1)
+            park_v(3)
+            park_u(4)
+            turn_x(0, 5)
+            copy_x(0, 5)
+            load_core(3, G)
+            nc.sync.dma_start(out=bias_sb[:], in_=bias.rearrange("(h p t) -> p h t", h=H, t=4))
+            nc.sync.dma_start(out=gain_sb[:], in_=gain.rearrange("(h p t) -> p h t", h=H, t=4))
+            load_vb(1)
+            load_ub(1, 0, 1)
+            load_ub(1, 1, 2)
+            load_ub(1, 2, G)
+            load_x(1)
+            interleave_w(0)
+            interleave_w(1)
+            nc.scalar.copy(out=gain32[:], in_=gain_sb[:])
             mult_z(0, 1, 7)
             permute_core(1, 0)
             quant_z(0, 1)
@@ -376,16 +381,15 @@ def tile_neural_tensor_pair_layer_g5_kernel(tc, u, v, core_words, core_scales, x
             permute_core(2, 0)
             quant_z(0, 2)
             permute_core(2, 1)
+            mult_z(0, 3)
             quant_x(0)
             quant_w(0)
-            mult_z(0, 3)
             permute_core(3, 0)
             quant_z(0, 3)
-            quant_w(1)
-            mult_z(1, 0)
             permute_core(3, 1)
+            mult_z(1, 0)
+            quant_w(1)
             quant_z(1, 0)
-            nc.scalar.copy(out=gain32[:], in_=gain_sb[:])
             for g in range(3):
                 for b in range(8):
                     mm_core(0, b // 4, b % 4, g, b, g == 0, False)
@@ -395,14 +399,16 @@ def tile_neural_tensor_pair_layer_g5_kernel(tc, u, v, core_words, core_scales, x
                 mm_core(0, 0, t, 3, t, False, True)
                 tanh(0, t, t)
             for t in range(4):
-                mm_x(0, 1, t, 4 + t, False, False)
+                mm_core(0, 1, t, 3, 4 + t, False, False)
             load_vb(2)
-            load_ub(2, 0, G)
+            load_ub(2, 0, 1)
+            load_ub(2, 1, G)
+            load_x(2)
             mult_z(1, 1)
             mult_z(1, 2)
             quant_z(1, 1)
             for t in range(4):
-                mm_core(0, 1, t, 3, 4 + t, False, True)
+                mm_x(0, 1, t, 4 + t, False, True)
                 tanh(1, t, 4 + t)
             mult_z(1, 3)
             quant_z(1, 2)
@@ -410,10 +416,10 @@ def tile_neural_tensor_pair_layer_g5_kernel(tc, u, v, core_words, core_scales, x
                 mm_core(1, 0, t, 0, t, True, False)
             turn_x(1, 4)
             copy_x(1, 4)
-            for t in range(4):
-                scale_s(0, t)
             quant_z(1, 3)
             quant_x(1)
+            for t in range(4):
+                scale_s(0, t)
             for g in range(1, G):
                 for t in range(4):
                     mm_core(1, 0, t, g, t, False, False)
@@ -443,25 +449,22 @@ def tile_neural_tensor_pair_layer_g5_kernel(tc, u, v, core_words, core_scales, x
             quant_z(2, 3)
             for t in range(1, 4):
                 scale(2, t)
-            interleave_y(0)
-            quant_x(2)
-            quant_y(0)
-            store_words(0)
             for j in range(4):
                 copy_y(1, j, "scalar")
+            quant_x(2)
             store_y(1, 0, 4)
+            interleave_y(0)
             for t in range(2, 4):
                 group(3, t)
                 tanh(3, t, t)
             turn_y(2, range(4))
-            interleave_y(1)
             for t in range(3):
                 scale(3, t)
-            quant_y(1)
-            scale(3, 3)
-            store_words(1)
+            quant_y(0)
+            store_words(0)
             for j in range(4):
                 copy_y(2, j, "scalar")
+            scale(3, 3)
             store_y(2, 0, 4)
             for t in range(2):
                 group(4, t)
@@ -470,26 +473,30 @@ def tile_neural_tensor_pair_layer_g5_kernel(tc, u, v, core_words, core_scales, x
             for j in range(4):
                 copy_y(3, j, "scalar")
             store_y(3, 0, 4)
+            interleave_y(1)
             interleave_y(2)
-            interleave_y(3)
+            quant_y(1)
             quant_y(2)
-            quant_y(3)
+            interleave_y(3)
+            store_words(1)
             store_words(2)
-            store_words(3)
-            store_scales(0, 2)
             for t in range(2, 4):
                 group(4, t)
                 tanh(4, t, t)
-            for t in range(4):
+            for t in range(3):
                 scale(4, t)
+            quant_y(3)
+            scale(4, 3)
+            store_words(3)
+            store_scales(0, 2)
             group(5, 0)
             tanh(5, 0, 0)
-            interleave_y(4)
             turn_y(4, range(4))
+            interleave_y(4)
             scale(5, 0)
             quant_y(4)
             for j in range(4):
-                copy_y(4, j, "scalar" if j % 2 else "vector")
+                copy_y(4, j, "scalar")
             store_words(4)
             store_y(4, 0, 4)
             group(5, 1)

@@ -19,10 +19,17 @@ COPY = mybir.ActivationFunctionType.Copy
 TANH = mybir.ActivationFunctionType.Tanh
 
 P = 128
+PACK = 4
 CH = 512
-NC = M // CH
-G = K // 512
-H = N // 512
+HALF = 512
+CHUNKS = M // CH
+PASSES = K // (P * PACK)
+HALVES = N // HALF
+UNITS = CHUNKS * HALVES
+TILES = CH // P
+Z_BUFS = 3
+OUT_BANK = 4
+U_PARK_ROWS, V_PARK_ROWS = 64, 16
 
 
 def tile_neural_tensor_pair_layer_g5_kernel(tc, u, v, core_words, core_scales, x, w, bias, gain, out_0, out_1, out_2):
@@ -37,154 +44,166 @@ def tile_neural_tensor_pair_layer_g5_kernel(tc, u, v, core_words, core_scales, x
         def tiles(name, count, shape, dtype):
             return [tile(name + str(k), shape, dtype) for k in range(count)]
 
-        bank = [ps.tile([P, 512], F32, name="bank" + str(k)) for k in range(8)]
+        bank = [ps.tile([P, CH], F32, name="bank" + str(k)) for k in range(8)]
         ident = tile("ident", [P, P], F32)
-        warm = tile("warm", [P, 1], F32)
-        idle_in = tile("idle_in", [P, 1024], BF16)
-        idle_codes = tile("idle_codes", [P, 256], U32)
-        idle_sc = tile("idle_sc", [P, 256], U8)
-        u_raw = tile("u_raw", [P, 12, I], BF16)
-        v_raw = tile("v_raw", [P, 12, J], BF16)
+
+        u_first = tile("u_first", [P, TILES, I], BF16)
+        v_first = tile("v_first", [P, TILES, J], BF16)
+        u_late = tile("u_late", [P, 4, 2, I], BF16)
+        v_late = tile("v_late", [P, 2 * TILES, J], BF16)
         u_in = tile("u_in", [P, 2, 2, P], F32)
         v_in = tile("v_in", [P, 2, P], F32)
         u_stage = tile("u_stage", [P, 2, 256], F32)
         v_stage = tile("v_stage", [P, P, 2], F32)
-        core_raw = tile("core_raw", [P, G, 2 * N], U8)
-        core = tile("core", [P, G, 2 * N], U8)
-        cs_raw = tile("cs_raw", [P, 512], U8)
-        cs_perm = tile("cs_perm", [P, 512], U8)
-        u_dup = tile("u_dup", [P, 4, I], F32)
-        cs = tile("cs", [P, G, N], U8)
-        w_il = tiles("w_il", H, [P, 2048], BF16)
-        w_codes = tiles("w_codes", H, [P, 512], U32)
-        w_sc = tiles("w_sc", H, [P, 512], U8)
-        x_raw = tiles("x_raw", NC, [P, 4, D], BF16)
-        x_il = tiles("x_il", 2, [P, 2048], BF16)
-        x_codes = tiles("x_codes", NC, [P, CH], U32)
-        x_sc = tiles("x_sc", NC, [P, CH], U8)
-        ub = tiles("ub", 2, [P, G, CH], F32)
-        vb = tiles("vb", 2, [P, 2 * CH], F32)
-        z = tiles("z", 3, [P, 2048], BF16)
-        z_codes = tiles("z_codes", 2, [P, G, CH], U32)
-        z_sc = tiles("z_sc", 2, [P, G, CH], U8)
-        bias_sb = tile("bias_sb", [P, H, 4], BF16)
-        gain_sb = tile("gain_sb", [P, H, 4], BF16)
-        gain32 = tile("gain32", [P, H, 4], F32)
-        y = tiles("y", 6, [P, 4, CH], F32)
-        y_il = tiles("y_il", 2, [P, 2048], BF16)
-        y_codes = tile("y_codes", [P, H, M], U32)
-        y_sc = tile("y_sc", [P, H, M], U8)
-        y_out = tiles("y_out", 2, [P, 4, 512], F32)
-        u_exp = y_out[1][:].rearrange("p g (j c) -> p g j c", j=4)
-        v_exp = y_out[0][:, 0:2, :].rearrange("p a (b e c) -> p (a b) e c", e=2, c=P)
-        w_raw = [y[5][:, 2 * h : 2 * h + 2, :].rearrange("p a c -> p (a c)").bitcast(BF16).rearrange("p (j n) -> p j n", j=4) for h in range(H)]
 
-        u_park = out_0[M - 80 : M - 16, :].rearrange("r n -> (r n)").rearrange("(c f) -> c f", c=2)
-        v_park = out_0[M - 16 : M, :].rearrange("r n -> (r n)")
+        core_raw = tile("core_raw", [P, PASSES, 2 * N], U8)
+        core = tile("core", [P, PASSES, 2 * N], U8)
+        cs_raw = tile("cs_raw", [P, HALF], U8)
+        cs_perm = tile("cs_perm", [P, HALF], U8)
+        u_dup = tile("u_dup", [P, TILES, I], F32)
+        cs = tile("cs", [P, PASSES, N], U8)
+        w_il = tiles("w_il", HALVES, [P, PACK * HALF], BF16)
+        w_codes = tiles("w_codes", HALVES, [P, HALF], U32)
+        w_sc = tiles("w_sc", HALVES, [P, HALF], U8)
+        x_raw = tiles("x_raw", CHUNKS, [P, TILES, D], BF16)
+        x_il = tiles("x_il", 2, [P, PACK * CH], BF16)
+        x_codes = tiles("x_codes", CHUNKS, [P, CH], U32)
+        x_sc = tiles("x_sc", CHUNKS, [P, CH], U8)
+        u_rep = tiles("u_rep", 2, [P, PASSES, CH], F32)
+        v_rep = tiles("v_rep", 2, [P, 2 * CH], F32)
+        z = tiles("z", Z_BUFS, [P, PACK * CH], BF16)
+        z_codes = tiles("z_codes", 2, [P, PASSES, CH], U32)
+        z_sc = tiles("z_sc", 2, [P, PASSES, CH], U8)
+        bias_sb = tile("bias_sb", [P, HALVES, PACK], BF16)
+        gain_sb = tile("gain_sb", [P, HALVES, PACK], BF16)
+        gain32 = tile("gain32", [P, HALVES, PACK], F32)
+        y = tiles("y", UNITS, [P, PACK, CH], F32)
+        y_il = tiles("y_il", 2, [P, PACK * CH], BF16)
+        y_codes = tile("y_codes", [P, HALVES, M], U32)
+        y_sc = tile("y_sc", [P, HALVES, M], U8)
+        y_out = tiles("y_out", 2, [P, TILES, HALF], F32)
+        u_exp = y_out[1][:].rearrange("p g (j c) -> p g j c", j=TILES)
+        v_exp = y_out[0][:, 0:2, :].rearrange("p a (b e c) -> p (a b) e c", e=2, c=P)
+        w_raw = y[UNITS - 1][:].bitcast(BF16)
+
+        u_rows = out_0[M - V_PARK_ROWS - U_PARK_ROWS : M - V_PARK_ROWS, :]
+        u_park = u_rows.rearrange("r n -> (r n)").rearrange("(c f) -> c f", c=2)
+        v_park = out_0[M - V_PARK_ROWS : M, :].rearrange("r n -> (r n)")
 
         def load_x(c):
-            nc.sync.dma_start(out=x_raw[c][:], in_=x[c * CH : (c + 1) * CH, :].rearrange("(j p) d -> p j d", p=P))
+            rows = x[c * CH : (c + 1) * CH, :].rearrange("(a p j) d -> p a j d", a=2, j=2)
+            nc.sync.dma_start(out=x_raw[c][:].rearrange("p (a j) d -> p a j d", a=2), in_=rows)
 
-        def load_w(h):
-            nc.sync.dma_start(out=w_raw[h][:], in_=w[:, h * 512 : (h + 1) * 512].rearrange("(p j) n -> p j n", j=4))
+        def load_first_uv():
+            rows = v[0:CH, :].rearrange("(a p j) i -> p a j i", a=2, j=2)
+            nc.sync.dma_start(out=v_first[:].rearrange("p (a j) i -> p a j i", a=2), in_=rows)
+            nc.sync.dma_start(out=u_first[:], in_=u[0:CH, :].rearrange("(j p) i -> p j i", p=P))
 
-        def load_u_raw(t0, t1):
-            nc.sync.dma_start(out=u_raw[:, t0:t1, :], in_=u[t0 * P : t1 * P, :].rearrange("(j p) i -> p j i", p=P))
+        def load_late_uv():
+            nc.sync.dma_start(out=v_late[:], in_=v[CH:M, :].rearrange("(j p) i -> p j i", p=P))
+            nc.sync.dma_start(out=u_late[:], in_=u[CH:M, :].rearrange("(a p j) i -> p a j i", a=4, j=2))
 
-        def load_core(g0, g1):
-            nc.sync.dma_start(out=core_raw[:, g0:g1, :].bitcast(I32), in_=core_words[g0:g1].rearrange("g p b -> p g b").bitcast(I32))
+        def load_core(g):
+            words = core_words[g : g + 1].rearrange("g p b -> p g b")
+            nc.sync.dma_start(out=core_raw[:, g : g + 1, :].bitcast(I32), in_=words.bitcast(I32))
 
-        def load_ub(c, g0, g1):
-            src = u_park[c - 1].rearrange("(i f) -> i f", i=16)[:, g0 * CH : g1 * CH]
-            nc.sync.dma_start(out=ub[c % 2][:, g0:g1, :].rearrange("p g m -> p (g m)"), in_=src.unsqueeze(1).to_broadcast([16, 8, (g1 - g0) * CH]))
+        def load_core_scales():
+            for h in range(HALVES):
+                rows = core_scales[:, :, h * HALF : (h + 1) * HALF].rearrange("g q n -> q g n")
+                nc.sync.dma_start(out=cs_raw[h:P:2, :].bitcast(I32), in_=rows.bitcast(I32))
 
-        def load_vb(c):
-            src = v_park[(c - 1) * 8 * 1024 : c * 8 * 1024].rearrange("(j f) -> j f", j=8)
-            nc.sync.dma_start(out=vb[c % 2][:], in_=src.unsqueeze(0).to_broadcast([16, 8, 1024]))
+        def load_u_rep(c, g0, g1):
+            rows = u_park[c - 1].rearrange("(i f) -> i f", i=16)[:, g0 * CH : g1 * CH]
+            dst = u_rep[c % 2][:, g0:g1, :].rearrange("p g m -> p (g m)")
+            nc.sync.dma_start(out=dst, in_=rows.unsqueeze(1).to_broadcast([16, 8, (g1 - g0) * CH]))
 
-        def load_v_raw(t0, t1):
-            nc.sync.dma_start(out=v_raw[:, t0:t1, :], in_=v[t0 * P : t1 * P, :].rearrange("(j p) i -> p j i", p=P))
+        def load_v_rep(c):
+            rows = v_park[(c - 1) * 16 * CH : c * 16 * CH].rearrange("(q f) -> q f", q=8)
+            nc.sync.dma_start(out=v_rep[c % 2][:], in_=rows.unsqueeze(0).to_broadcast([16, 8, 2 * CH]))
 
         def expand_v():
-            words = v_raw[:, 0:4, :].bitcast(F32).rearrange("p j (q e) -> p j e q", e=2)
+            words = v_first[:].bitcast(F32).rearrange("p j (q e) -> p j e q", e=2)
             nc.vector.tensor_copy(
                 out=v_exp[:].rearrange("p j e (r q) -> p j e r q", q=8),
-                in_=words.unsqueeze(3).to_broadcast([P, 4, 2, 16, 8]),
+                in_=words.unsqueeze(3).to_broadcast([P, TILES, 2, 16, 8]),
             )
 
-        def turn_v(b0):
-            for j in range(4):
+        def turn_words(words, b0):
+            for j in range(TILES):
                 for e in range(2):
                     col = (2 * (j % 2) + e) * P
-                    nc.tensor.transpose(bank[b0 + j // 2][:, col : col + P], v_exp[:, j, e, :], ident[:])
+                    nc.tensor.transpose(bank[b0 + j // 2][:, col : col + P], words(j, e), ident[:])
 
-        def copy_pairs(dst, b0):
-            dst = dst.rearrange("p (j m e) -> p j m e", j=4, e=2)
+        def copy_words(dst, b0):
+            dst = dst.rearrange("p (a m r) -> p a m r", a=2, r=4)
             for a in range(2):
-                nc.scalar.copy(out=dst[:, 2 * a : 2 * a + 2], in_=bank[b0 + a][:].rearrange("p (j e m) -> p j m e", j=2, e=2))
+                nc.scalar.copy(out=dst[:, a], in_=bank[b0 + a][:].rearrange("p (r m) -> p m r", r=4))
 
         def double_u():
             nc.vector.tensor_copy(
                 out=u_dup[:].bitcast(BF16).rearrange("p j (i d) -> p j i d", d=2),
-                in_=u_raw[:, 0:4, :].unsqueeze(3).to_broadcast([P, 4, I, 2]),
+                in_=u_first[:].unsqueeze(3).to_broadcast([P, TILES, I, 2]),
             )
 
         def expand_u(g):
             nc.vector.tensor_copy(
                 out=u_exp[:, g].rearrange("p j (i r) -> p j i r", r=8),
-                in_=u_dup[:, :, 16 * g : 16 * g + 16].unsqueeze(3).to_broadcast([P, 4, 16, 8]),
+                in_=u_dup[:, :, 16 * g : 16 * g + 16].unsqueeze(3).to_broadcast([P, TILES, 16, 8]),
             )
 
-        def turn_u0(g, b):
-            for j in range(4):
+        def turn_u(g, b):
+            for j in range(TILES):
                 nc.tensor.transpose(bank[b][:, j * P : (j + 1) * P], u_exp[:, g, j, :], ident[:])
 
         def order_v():
-            words = v_raw[:, 4:12, :].bitcast(F32).rearrange("p (c j) (q e) -> p e c q j", j=4, e=2)
+            words = v_late[:].bitcast(F32).rearrange("p (c j) (q e) -> p e c q j", j=TILES, e=2)
             for e in range(2):
-                nc.scalar.copy(out=v_in[:, e, 0:64].rearrange("p (c q j) -> p c q j", c=2, j=4), in_=words[:, e])
+                nc.scalar.copy(out=v_in[:, e, 0:64].rearrange("p (c q j) -> p c q j", c=2, j=TILES), in_=words[:, e])
 
         def order_u(c):
-            for jj in range(2):
-                src = u_raw[:, 4 * c + jj : 4 * c + 4 : 2, :].rearrange("p a (g i) -> p i g a", i=16)
-                dst = u_in[:, c - 1, jj, :].bitcast(BF16).rearrange("p (i g a d) -> p i g a d", g=G, a=2, d=2)
-                nc.scalar.copy(out=dst, in_=src.unsqueeze(4).to_broadcast([P, 16, G, 2, 2]))
+            for j in range(2):
+                src = u_late[:, 2 * c - 2 : 2 * c, j, :].rearrange("p a (g i) -> p i g a", i=16)
+                dst = u_in[:, c - 1, j, :].bitcast(BF16).rearrange("p (i g a d) -> p i g a d", g=PASSES, a=2, d=2)
+                nc.scalar.copy(out=dst, in_=src.unsqueeze(4).to_broadcast([P, 16, PASSES, 2, 2]))
 
-        def turn_parked_v(b):
+        def turn_late_v(b):
             for e in range(2):
                 nc.tensor.transpose(bank[b][:, e * P : (e + 1) * P], v_in[:, e, :], ident[:])
+
+        def turn_late_u(b):
+            for k in range(4):
+                nc.tensor.transpose(bank[b][:, k * P : (k + 1) * P], u_in[:, k // 2, k % 2, :], ident[:])
 
         def park_v(b):
             nc.scalar.copy(out=v_stage[0:64], in_=bank[b][0:64, 0:256].rearrange("p (e m) -> p m e", e=2))
             nc.sync.dma_start(out=v_park.rearrange("(p f) -> p f", p=64), in_=v_stage[0:64].rearrange("p m e -> p (m e)"))
 
-        def turn_parked_u(b):
-            for k in range(4):
-                nc.tensor.transpose(bank[b][:, k * P : (k + 1) * P], u_in[:, k // 2, k % 2, :], ident[:])
-
         def park_u(b):
-            nc.scalar.copy(out=u_stage[:].rearrange("p c f -> p (c f)"), in_=bank[b][:])
+            nc.scalar.copy(
+                out=u_stage[:].rearrange("p c (m j) -> p c m j", j=2),
+                in_=bank[b][:].rearrange("p (c j m) -> p c m j", c=2, j=2),
+            )
             nc.sync.dma_start(out=u_park.rearrange("c (p f) -> p c f", p=P), in_=u_stage[:])
 
         def permute_core(g, h):
-            cols = slice(h * 1024, (h + 1) * 1024)
+            cols = slice(2 * h * HALF, 2 * (h + 1) * HALF)
             nc.vector.tensor_copy(
-                out=core[:, g, cols].rearrange("p (t m b) -> p t m b", t=4, b=2),
-                in_=core_raw[:, g, cols].rearrange("p (m t b) -> p t m b", t=4, b=2),
+                out=core[:, g, cols].rearrange("p (t m b) -> p t m b", t=PACK, b=2),
+                in_=core_raw[:, g, cols].rearrange("p (m t b) -> p t m b", t=PACK, b=2),
             )
 
-        def permute_scales():
+        def permute_core_scales():
             nc.vector.tensor_copy(
-                out=cs_perm[:].rearrange("p (t m) -> p t m", t=4),
-                in_=cs_raw[:].rearrange("p (m t) -> p t m", t=4),
+                out=cs_perm[:].rearrange("p (t m) -> p t m", t=PACK),
+                in_=cs_raw[:].rearrange("p (m t) -> p t m", t=PACK),
             )
             for q in range(4):
                 nc.scalar.dma_start(out=cs[32 * q : 32 * q + 4].bitcast(I32), in_=cs_perm[32 * q : 32 * q + 32, :].bitcast(I32))
 
         def interleave_w(h):
             nc.scalar.copy(
-                out=w_il[h][:].rearrange("p (t m j) -> p t m j", t=4, j=4),
-                in_=w_raw[h][:].rearrange("p j (m t) -> p t m j", t=4),
+                out=w_il[h][:].rearrange("p (t m j) -> p t m j", t=PACK, j=PACK),
+                in_=w_raw[:, :, h * HALF : (h + 1) * HALF].rearrange("p j (m t) -> p t m j", t=PACK),
             )
 
         def quantize(codes, scales, src):
@@ -195,284 +214,261 @@ def tile_neural_tensor_pair_layer_g5_kernel(tc, u, v, core_words, core_scales, x
 
         def turn_x(c, b0):
             words = x_raw[c][:].bitcast(F32)
-            for j in range(4):
-                for e in range(2):
-                    col = (2 * (j % 2) + e) * P
-                    src = words[:, j, e:256:2]
-                    nc.tensor.transpose(bank[b0 + j // 2][:, col : col + P], src, ident[:])
-
-        def copy_x(c, b0):
-            copy_pairs(x_il[c % 2][:].bitcast(F32), b0)
+            turn_words(lambda j, e: words[:, j, e : 2 * P : 2], b0)
+            copy_words(x_il[c % 2][:].bitcast(F32), b0)
 
         def quant_x(c):
             quantize(x_codes[c][:], x_sc[c][:], x_il[c % 2][:])
 
-        def mult_z(c, g, b=None, m0=0, m1=CH):
-            src = ub[c % 2][:, g, m0:m1] if b is None else bank[b][:, m0:m1]
-            pair = src.bitcast(BF16).rearrange("p (m d) -> p m d", d=2)
+        def mult_z(c, g, u_words):
+            pairs = u_words.bitcast(BF16).rearrange("p (m d) -> p m d", d=2)
             nc.vector.tensor_tensor(
-                out=z[(G * c + g) % 3][:, 4 * m0 : 4 * m1].rearrange("p (m a d) -> p m a d", a=2, d=2),
-                in0=vb[c % 2][:, 2 * m0 : 2 * m1].bitcast(BF16).rearrange("p (m a d) -> p m a d", a=2, d=2),
-                in1=pair.unsqueeze(2).to_broadcast([P, m1 - m0, 2, 2]),
+                out=z[(PASSES * c + g) % Z_BUFS][:].rearrange("p (m e d) -> p m e d", e=2, d=2),
+                in0=v_rep[c % 2][:].bitcast(BF16).rearrange("p (m e d) -> p m e d", e=2, d=2),
+                in1=pairs.unsqueeze(2).to_broadcast([P, CH, 2, 2]),
                 op=MULT,
             )
 
-        def quant_z(c, g):
-            quantize(z_codes[c % 2][:, g, :], z_sc[c % 2][:, g, :], z[(G * c + g) % 3][:])
+        def mult_z_sbuf(c, g):
+            mult_z(c, g, u_rep[c % 2][:, g, :])
 
-        def mm_core(c, h, t, g, b, start, stop):
-            col = h * 512 + t * P
+        def quant_z(c, g):
+            quantize(z_codes[c % 2][:, g, :], z_sc[c % 2][:, g, :], z[(PASSES * c + g) % Z_BUFS][:])
+
+        def mm_core(n, t, g, b, start, stop, m0=0, m1=CH):
+            c, h = divmod(n, HALVES)
+            col = h * HALF + t * P
             nc.tensor.matmul_mx(
-                out=bank[b][:],
-                lhsT=core[:, g, 2 * col : 2 * col + 2 * P].bitcast(FP4X4),
+                out=bank[b][:, m0:m1],
+                lhsT=core[:, g, 2 * col : 2 * (col + P)].bitcast(FP4X4),
                 lhsT_scale=cs[:, g, col : col + P],
-                rhs=z_codes[c % 2][:, g, :].bitcast(FP8X4),
-                rhs_scale=z_sc[c % 2][:, g, :],
+                rhs=z_codes[c % 2][:, g, m0:m1].bitcast(FP8X4),
+                rhs_scale=z_sc[c % 2][:, g, m0:m1],
                 start=start,
                 stop=stop,
             )
 
-        def mm_x(c, h, t, b, start, stop):
+        def mm_x(n, t, b, start, stop, m0=0, m1=CH):
+            c, h = divmod(n, HALVES)
             nc.tensor.matmul_mx(
-                out=bank[b][:],
+                out=bank[b][:, m0:m1],
                 lhsT=w_codes[h][:, t * P : (t + 1) * P].bitcast(FP8X4),
                 lhsT_scale=w_sc[h][:, t * P : (t + 1) * P],
-                rhs=x_codes[c][:].bitcast(FP8X4),
-                rhs_scale=x_sc[c][:],
+                rhs=x_codes[c][:, m0:m1].bitcast(FP8X4),
+                rhs_scale=x_sc[c][:, m0:m1],
                 start=start,
                 stop=stop,
             )
 
-        def keep_warm(count, b):
-            for k in range(count):
-                nc.tensor.matmul_mx(out=bank[b][:, 0:256], lhsT=idle_codes[:, 0:P].bitcast(FP8X4), lhsT_scale=idle_sc[:, 0:P],
-                                    rhs=idle_codes[:].bitcast(FP8X4), rhs_scale=idle_sc[:], start=True, stop=True)
-
-        def quarter_group(n, t, j, b):
-            c, h = divmod(n, H)
-            col = h * 512 + t * P
-            tok = slice(j * P, (j + 1) * P)
-            nc.tensor.matmul_mx(out=bank[b][:, tok], lhsT=w_codes[h][:, t * P : (t + 1) * P].bitcast(FP8X4), lhsT_scale=w_sc[h][:, t * P : (t + 1) * P],
-                                rhs=x_codes[c][:, tok].bitcast(FP8X4), rhs_scale=x_sc[c][:, tok], start=True, stop=False)
-            for g in range(G):
-                nc.tensor.matmul_mx(out=bank[b][:, tok], lhsT=core[:, g, 2 * col : 2 * col + 2 * P].bitcast(FP4X4), lhsT_scale=cs[:, g, col : col + P],
-                                    rhs=z_codes[c % 2][:, g, tok].bitcast(FP8X4), rhs_scale=z_sc[c % 2][:, g, tok], start=False, stop=g == G - 1)
-
-        def group(n, t):
-            c, h = divmod(n, H)
-            mm_x(c, h, t, t, True, False)
-            for g in range(G):
-                mm_core(c, h, t, g, t, False, g == G - 1)
-
         def tanh(n, t, b, m0=0, m1=CH):
-            nc.scalar.activation(out=y[n][:, t, m0:m1], in_=bank[b][:, m0:m1], func=TANH, bias=bias_sb[:, n % H, t : t + 1])
+            nc.scalar.activation(out=y[n][:, t, m0:m1], in_=bank[b][:, m0:m1], func=TANH, bias=bias_sb[:, n % HALVES, t : t + 1])
 
-        def scale_s(n, t):
-            nc.scalar.activation(out=y[n][:, t, :], in_=y[n][:, t, :], func=COPY, scale=gain32[:, n % H, t : t + 1])
+        def group(n, t, b, m0=0, m1=CH):
+            mm_x(n, t, b, True, False, m0, m1)
+            for g in range(PASSES):
+                mm_core(n, t, g, b, False, g == PASSES - 1, m0, m1)
+            tanh(n, t, b, m0, m1)
 
-        def scale(n, t, m0=0, m1=CH):
-            nc.vector.tensor_scalar(out=y[n][:, t, m0:m1], in0=y[n][:, t, m0:m1], scalar1=gain_sb[:, n % H, t : t + 1], scalar2=None, op0=MULT)
+        def gain_on_scalar(n, t):
+            nc.scalar.activation(out=y[n][:, t, :], in_=y[n][:, t, :], func=COPY, scale=gain32[:, n % HALVES, t : t + 1])
+
+        def gain_on_vector(n, t, m0=0, m1=CH):
+            rows = y[n][:, t, m0:m1]
+            nc.vector.tensor_scalar(out=rows, in0=rows, scalar1=gain_sb[:, n % HALVES, t : t + 1], scalar2=None, op0=MULT)
 
         def interleave_y(n, m0=0, m1=CH):
             nc.vector.tensor_copy(
-                out=y_il[n % 2][:, 4 * m0 : 4 * m1].rearrange("p (m t) -> p m t", t=4),
+                out=y_il[n % 2][:, PACK * m0 : PACK * m1].rearrange("p (m t) -> p m t", t=PACK),
                 in_=y[n][:, :, m0:m1].rearrange("p t m -> p m t"),
             )
 
         def quant_y(n, m0=0, m1=CH):
-            c, h = divmod(n, H)
+            c, h = divmod(n, HALVES)
             cols = slice(c * CH + m0, c * CH + m1)
-            quantize(y_codes[:, h, cols], y_sc[:, h, cols], y_il[n % 2][:, 4 * m0 : 4 * m1])
+            quantize(y_codes[:, h, cols], y_sc[:, h, cols], y_il[n % 2][:, PACK * m0 : PACK * m1])
 
         def store_words(n):
-            c, h = divmod(n, H)
+            c, h = divmod(n, HALVES)
             cols = slice(c * CH, (c + 1) * CH)
-            nc.sync.dma_start(out=out_1[h, :, cols, :].rearrange("p m t -> p (m t)").bitcast(I32), in_=y_codes[:, h, cols].bitcast(I32))
+            dst = out_1[h, :, cols, :].rearrange("p m t -> p (m t)")
+            nc.sync.dma_start(out=dst.bitcast(I32), in_=y_codes[:, h, cols].bitcast(I32))
 
         def store_scales(c0, c1):
             cols = slice(c0 * CH, c1 * CH)
             for q in range(4):
-                nc.sync.dma_start(
-                    out=out_2[:, 4 * q : 4 * q + 4, cols].rearrange("h r m -> r h m").bitcast(I32),
-                    in_=y_sc[32 * q : 32 * q + 4, :, cols].bitcast(I32),
-                )
+                dst = out_2[:, 4 * q : 4 * q + 4, cols].rearrange("h r m -> r h m")
+                nc.sync.dma_start(out=dst.bitcast(I32), in_=y_sc[32 * q : 32 * q + 4, :, cols].bitcast(I32))
 
-        def turn_y(n, ts, js=range(4)):
-            for j in js:
-                for t in ts:
-                    nc.tensor.transpose(bank[4 + j][:, t * P : (t + 1) * P], y[n][:, t, j * P : (j + 1) * P], ident[:])
+        def turn_y(n, j0, j1):
+            for j in range(j0, j1):
+                for t in range(PACK):
+                    nc.tensor.transpose(bank[OUT_BANK + j][:, t * P : (t + 1) * P], y[n][:, t, j * P : (j + 1) * P], ident[:])
 
-        def copy_y(n, j, engine):
-            dst = y_out[n % 2][:, j, :].rearrange("m (p t) -> m p t", t=4)
-            src = bank[4 + j][:].rearrange("m (t p) -> m p t", t=4)
-            if engine == "vector":
-                nc.vector.tensor_copy(out=dst, in_=src)
-            else:
-                nc.scalar.copy(out=dst, in_=src)
+        def copy_y(n, j, copy):
+            copy(
+                out=y_out[n % 2][:, j, :].rearrange("m (p t) -> m p t", t=PACK),
+                in_=bank[OUT_BANK + j][:].rearrange("m (t p) -> m p t", t=PACK),
+            )
 
         def store_y(n, j0, j1):
-            c, h = divmod(n, H)
-            rows = out_0[c * CH + j0 * P : c * CH + j1 * P, h * 512 : (h + 1) * 512]
+            c, h = divmod(n, HALVES)
+            rows = out_0[c * CH + j0 * P : c * CH + j1 * P, h * HALF : (h + 1) * HALF]
             nc.sync.dma_start(out=rows.rearrange("(j m) n -> m j n", m=P), in_=y_out[n % 2][:, j0:j1, :])
 
+        def empty_out_banks(n):
+            for j in range(TILES):
+                copy_y(n, j, nc.scalar.copy)
+
         with tc.manual_schedule():
-            nc.vector.memset(idle_in[:].bitcast(I32), 0)
-            nc.vector.memset(v_in[:, :, 64:P], 0.0)
-            quantize(idle_codes[:], idle_sc[:], idle_in[:])
             nc.vector.memset(cs[:].rearrange("p g n -> p (g n)").bitcast(I32), 0)
             make_identity(nc, ident[:])
-            nc.scalar.activation(out=warm[:], in_=v_in[:, 0, 64:65], func=TANH)
-            keep_warm(7, 7)
-            load_v_raw(0, 4)
-            load_u_raw(0, 4)
-            for h in range(H):
-                nc.sync.dma_start(out=cs_raw[h:P:2, :].bitcast(I32), in_=core_scales[:, :, h * 512 : (h + 1) * 512].rearrange("g q n -> q g n").bitcast(I32))
-            load_core(0, 1)
-            load_v_raw(4, 12)
-            load_u_raw(4, 12)
+            nc.scalar.activation(out=v_in[:, :, 64:P], in_=ident[:].rearrange("p (e c) -> p e c", e=2), func=TANH)
+            load_first_uv()
+            load_core_scales()
+            load_core(0)
+            load_late_uv()
             load_x(0)
-            load_core(1, 2)
+            load_core(1)
+
             expand_v()
             double_u()
-            permute_scales()
-            turn_v(5)
-            copy_pairs(vb[0][:], 5)
-            keep_warm(5, 3)
-            load_w(0)
-            load_core(2, 3)
+            permute_core_scales()
+            turn_words(lambda j, e: v_exp[:, j, e, :], 5)
+            copy_words(v_rep[0][:], 5)
+            nc.sync.dma_start(out=w_raw, in_=w.rearrange("(p j) n -> p j n", j=PACK))
+            load_core(2)
+            expand_u(0)
+            expand_u(1)
             permute_core(0, 0)
-            for g in range(G):
-                expand_u(g)
-            turn_u0(0, 0)
-            turn_u0(1, 7)
+            expand_u(2)
+            expand_u(3)
+            turn_u(0, 0)
+            turn_u(1, 7)
             order_v()
             order_u(1)
             order_u(2)
-            turn_u0(2, 1)
-            turn_u0(3, 2)
-            turn_parked_v(3)
-            turn_parked_u(4)
-            mult_z(0, 0, 0)
+            turn_u(2, 1)
+            turn_u(3, 2)
+            turn_late_v(3)
+            turn_late_u(4)
+            mult_z(0, 0, bank[0][:])
             permute_core(0, 1)
             quant_z(0, 0)
-            for g in range(2, G):
-                nc.scalar.copy(out=ub[0][:, g, :], in_=bank[g - 1][:])
-            load_w(1)
+            for g in (2, 3):
+                nc.scalar.copy(out=u_rep[0][:, g, :], in_=bank[g - 1][:])
             park_v(3)
             park_u(4)
+            for b in range(5):
+                mm_core(b // PACK, b % PACK, 0, b, True, False)
             turn_x(0, 5)
-            copy_x(0, 5)
-            load_core(3, G)
-            nc.sync.dma_start(out=bias_sb[:], in_=bias.rearrange("(h p t) -> p h t", h=H, t=4))
-            nc.sync.dma_start(out=gain_sb[:], in_=gain.rearrange("(h p t) -> p h t", h=H, t=4))
-            load_vb(1)
-            load_ub(1, 0, 1)
-            load_ub(1, 1, 2)
-            load_ub(1, 2, G)
+            load_core(3)
+            nc.sync.dma_start(out=bias_sb[:], in_=bias.rearrange("(h p t) -> p h t", h=HALVES, t=PACK))
+            nc.sync.dma_start(out=gain_sb[:], in_=gain.rearrange("(h p t) -> p h t", h=HALVES, t=PACK))
+            load_v_rep(1)
+            load_u_rep(1, 0, 1)
+            load_u_rep(1, 1, 2)
+            load_u_rep(1, 2, PASSES)
             load_x(1)
             interleave_w(0)
             interleave_w(1)
             nc.scalar.copy(out=gain32[:], in_=gain_sb[:])
-            mult_z(0, 1, 7)
+
+            mult_z(0, 1, bank[7][:])
             permute_core(1, 0)
             quant_z(0, 1)
             permute_core(1, 1)
-            mult_z(0, 2)
+            mult_z_sbuf(0, 2)
             permute_core(2, 0)
             quant_z(0, 2)
             permute_core(2, 1)
-            mult_z(0, 3)
+            mult_z_sbuf(0, 3)
             quant_x(0)
             quant_w(0)
             permute_core(3, 0)
             quant_z(0, 3)
             permute_core(3, 1)
-            mult_z(1, 0)
+            mult_z_sbuf(1, 0)
             quant_w(1)
             quant_z(1, 0)
-            for g in range(3):
-                for b in range(8):
-                    mm_core(0, b // 4, b % 4, g, b, g == 0, False)
-            for t in range(4):
-                mm_x(0, 0, t, t, False, False)
-            for t in range(4):
-                mm_core(0, 0, t, 3, t, False, True)
+            mm_core(1, 3, 0, 7, True, False)
+            for b in (0, 1, 2, 3, 4, 7):
+                mm_core(b // PACK, b % PACK, 1, b, False, False)
+            for g in (0, 1):
+                for b in (5, 6):
+                    mm_core(1, b % PACK, g, b, g == 0, False)
+            for b in range(2 * PACK):
+                mm_core(b // PACK, b % PACK, 2, b, False, False)
+            for t in range(PACK):
+                mm_x(0, t, t, False, False)
+            for t in range(PACK):
+                mm_core(0, t, PASSES - 1, t, False, True)
                 tanh(0, t, t)
-            for t in range(4):
-                mm_core(0, 1, t, 3, 4 + t, False, False)
-            load_vb(2)
-            load_ub(2, 0, 1)
-            load_ub(2, 1, G)
+            for t in range(PACK):
+                mm_core(1, t, PASSES - 1, PACK + t, False, False)
+            load_v_rep(2)
+            load_u_rep(2, 0, 1)
+            load_u_rep(2, 1, PASSES)
             load_x(2)
-            mult_z(1, 1)
-            mult_z(1, 2)
+            mult_z_sbuf(1, 1)
+            mult_z_sbuf(1, 2)
             quant_z(1, 1)
-            for t in range(4):
-                mm_x(0, 1, t, 4 + t, False, True)
-                tanh(1, t, 4 + t)
-            mult_z(1, 3)
+            for t in range(PACK):
+                mm_x(1, t, PACK + t, False, True)
+                tanh(1, t, PACK + t)
+            mult_z_sbuf(1, 3)
             quant_z(1, 2)
-            for t in range(4):
-                mm_core(1, 0, t, 0, t, True, False)
-            turn_x(1, 4)
-            copy_x(1, 4)
+
+            for t in range(PACK):
+                mm_core(2, t, 0, t, True, False)
+            turn_x(1, OUT_BANK)
             quant_z(1, 3)
             quant_x(1)
-            for t in range(4):
-                scale_s(0, t)
-            for g in range(1, G):
-                for t in range(4):
-                    mm_core(1, 0, t, g, t, False, False)
-            for t in range(4):
-                mm_x(1, 0, t, t, False, True)
+            for t in range(PACK):
+                gain_on_scalar(0, t)
+            for g in range(1, PASSES):
+                for t in range(PACK):
+                    mm_core(2, t, g, t, False, False)
+            for t in range(PACK):
+                mm_x(2, t, t, False, True)
                 tanh(2, t, t)
-            turn_y(0, range(4))
-            for t in range(4):
-                scale(1, t)
-            mult_z(2, 0)
-            mult_z(2, 1)
-            quant_z(2, 0)
-            mult_z(2, 2)
-            quant_z(2, 1)
-            mult_z(2, 3)
-            quant_z(2, 2)
-            for j in range(4):
-                copy_y(0, j, "scalar")
-            store_y(0, 0, 4)
-            for t in range(2):
-                group(3, t)
-                tanh(3, t, t)
+            turn_y(0, 0, TILES)
+            for t in range(PACK):
+                gain_on_vector(1, t)
+            mult_z_sbuf(2, 0)
+            for g in range(1, PASSES):
+                mult_z_sbuf(2, g)
+                quant_z(2, g - 1)
+            empty_out_banks(0)
+            store_y(0, 0, TILES)
+
+            for t in (0, 1):
+                group(3, t, t)
             turn_x(2, 2)
-            copy_x(2, 2)
-            turn_y(1, range(4))
-            scale(2, 0)
-            quant_z(2, 3)
-            for t in range(1, 4):
-                scale(2, t)
-            for j in range(4):
-                copy_y(1, j, "scalar")
+            turn_y(1, 0, TILES)
+            gain_on_vector(2, 0)
+            quant_z(2, PASSES - 1)
+            for t in range(1, PACK):
+                gain_on_vector(2, t)
+            empty_out_banks(1)
             quant_x(2)
-            store_y(1, 0, 4)
+            store_y(1, 0, TILES)
             interleave_y(0)
-            for t in range(2, 4):
-                group(3, t)
-                tanh(3, t, t)
-            turn_y(2, range(4))
-            for t in range(3):
-                scale(3, t)
+            for t in (2, 3):
+                group(3, t, t)
+            turn_y(2, 0, TILES)
+            for t in range(PACK - 1):
+                gain_on_vector(3, t)
             quant_y(0)
             store_words(0)
-            for j in range(4):
-                copy_y(2, j, "scalar")
-            scale(3, 3)
-            store_y(2, 0, 4)
-            for t in range(2):
-                group(4, t)
-                tanh(4, t, t)
-            turn_y(3, range(4))
-            for j in range(4):
-                copy_y(3, j, "scalar")
-            store_y(3, 0, 4)
+            empty_out_banks(2)
+            gain_on_vector(3, PACK - 1)
+            store_y(2, 0, TILES)
+
+            for t in (0, 1):
+                group(4, t, t)
+            turn_y(3, 0, TILES)
+            empty_out_banks(3)
+            store_y(3, 0, TILES)
             interleave_y(1)
             interleave_y(2)
             quant_y(1)
@@ -480,47 +476,44 @@ def tile_neural_tensor_pair_layer_g5_kernel(tc, u, v, core_words, core_scales, x
             interleave_y(3)
             store_words(1)
             store_words(2)
-            for t in range(2, 4):
-                group(4, t)
-                tanh(4, t, t)
-            for t in range(3):
-                scale(4, t)
+            for t in (2, 3):
+                group(4, t, t)
+            for t in range(PACK - 1):
+                gain_on_vector(4, t)
             quant_y(3)
-            scale(4, 3)
+            gain_on_vector(4, PACK - 1)
             store_words(3)
             store_scales(0, 2)
-            group(5, 0)
-            tanh(5, 0, 0)
-            turn_y(4, range(4))
+
+            last = UNITS - 1
+            group(last, 0, 0)
+            turn_y(4, 0, TILES)
             interleave_y(4)
-            scale(5, 0)
+            gain_on_vector(last, 0)
             quant_y(4)
-            for j in range(4):
-                copy_y(4, j, "scalar")
+            empty_out_banks(4)
             store_words(4)
-            store_y(4, 0, 4)
-            group(5, 1)
-            tanh(5, 1, 1)
-            scale(5, 1)
-            for j in range(4):
-                for t in range(2, 4):
-                    b = (2, 3, 0, 1)[2 * (j % 2) + t - 2]
-                    quarter_group(5, t, j, b)
-                    tanh(5, t, b, j * P, j * P + P)
-                    scale(5, t, j * P, j * P + P)
-                if j == 2:
-                    turn_y(5, range(4), [0, 1])
-                    interleave_y(5, 0, 256)
-                    copy_y(5, 0, "scalar")
-                    copy_y(5, 1, "vector")
-                    store_y(5, 0, 2)
-            turn_y(5, range(4), [2, 3])
-            quant_y(5, 0, 256)
-            interleave_y(5, 256, 512)
-            copy_y(5, 2, "scalar")
-            store_y(5, 2, 3)
-            quant_y(5, 256, 512)
-            copy_y(5, 3, "scalar")
-            store_y(5, 3, 4)
-            store_words(5)
-            store_scales(2, 3)
+            store_y(4, 0, TILES)
+            group(last, 1, 1)
+            gain_on_vector(last, 1)
+
+            for j in range(TILES):
+                for t in (2, 3):
+                    group(last, t, (2 * j + t) % PACK, j * P, (j + 1) * P)
+                    gain_on_vector(last, t, j * P, (j + 1) * P)
+                if j == TILES - 2:
+                    turn_y(last, 0, 2)
+                    copy_y(last, 0, nc.scalar.copy)
+                    copy_y(last, 1, nc.vector.tensor_copy)
+                    store_y(last, 0, 2)
+                    interleave_y(last, 0, CH // 2)
+            turn_y(last, 2, TILES)
+            quant_y(last, 0, CH // 2)
+            interleave_y(last, CH // 2, CH)
+            copy_y(last, 2, nc.scalar.copy)
+            store_y(last, 2, 3)
+            quant_y(last, CH // 2, CH)
+            copy_y(last, 3, nc.scalar.copy)
+            store_y(last, 3, TILES)
+            store_scales(2, CHUNKS)
+            store_words(last)

from contextlib import ExitStack

import concourse.mybir as mybir
from concourse.masks import make_identity

M, I, J, D, N = 1536, 64, 32, 512, 1024
K = I * J
FLOPS = 2 * M * (K + D) * N

F32 = mybir.dt.float32
BF16 = mybir.dt.bfloat16
I32 = mybir.dt.int32
U32 = mybir.dt.uint32
U8 = mybir.dt.uint8
FP8X4 = mybir.dt.float8_e4m3fn_x4
FP4X4 = mybir.dt.float4_e2m1fn_x4
MULT = mybir.AluOpType.mult
COPY = mybir.ActivationFunctionType.Copy
TANH = mybir.ActivationFunctionType.Tanh

P = 128
PACK = 4
CH = 512
HALF = 512
CHUNKS = M // CH
PASSES = K // (P * PACK)
HALVES = N // HALF
UNITS = CHUNKS * HALVES
TILES = CH // P
Z_BUFS = 3
OUT_BANK = 4
U_PARK_ROWS, V_PARK_ROWS = 64, 16


def tile_neural_tensor_pair_layer_g5_kernel(tc, u, v, core_words, core_scales, x, w, bias, gain, out_0, out_1, out_2):
    nc = tc.nc
    with ExitStack() as ctx:
        sb = ctx.enter_context(tc.tile_pool(name="sb", bufs=1))
        ps = ctx.enter_context(tc.psum_pool(name="ps", bufs=1))

        def tile(name, shape, dtype):
            return sb.tile(shape, dtype, name=name, align_bytes=256)

        def tiles(name, count, shape, dtype):
            return [tile(name + str(k), shape, dtype) for k in range(count)]

        bank = [ps.tile([P, CH], F32, name="bank" + str(k)) for k in range(8)]
        ident = tile("ident", [P, P], F32)

        u_first = tile("u_first", [P, TILES, I], BF16)
        v_first = tile("v_first", [P, TILES, J], BF16)
        u_late = tile("u_late", [P, 4, 2, I], BF16)
        v_late = tile("v_late", [P, 2 * TILES, J], BF16)
        u_in = tile("u_in", [P, 2, 2, P], F32)
        v_in = tile("v_in", [P, 2, P], F32)
        u_stage = tile("u_stage", [P, 2, 256], F32)
        v_stage = tile("v_stage", [P, P, 2], F32)

        core_raw = tile("core_raw", [P, PASSES, 2 * N], U8)
        core = tile("core", [P, PASSES, 2 * N], U8)
        cs_raw = tile("cs_raw", [P, HALF], U8)
        cs_perm = tile("cs_perm", [P, HALF], U8)
        u_dup = tile("u_dup", [P, TILES, I], F32)
        cs = tile("cs", [P, PASSES, N], U8)
        w_il = tiles("w_il", HALVES, [P, PACK * HALF], BF16)
        w_codes = tiles("w_codes", HALVES, [P, HALF], U32)
        w_sc = tiles("w_sc", HALVES, [P, HALF], U8)
        x_raw = tiles("x_raw", CHUNKS, [P, TILES, D], BF16)
        x_il = tiles("x_il", 2, [P, PACK * CH], BF16)
        x_codes = tiles("x_codes", CHUNKS, [P, CH], U32)
        x_sc = tiles("x_sc", CHUNKS, [P, CH], U8)
        u_rep = tiles("u_rep", 2, [P, PASSES, CH], F32)
        v_rep = tiles("v_rep", 2, [P, 2 * CH], F32)
        z = tiles("z", Z_BUFS, [P, PACK * CH], BF16)
        z_codes = tiles("z_codes", 2, [P, PASSES, CH], U32)
        z_sc = tiles("z_sc", 2, [P, PASSES, CH], U8)
        bias_sb = tile("bias_sb", [P, HALVES, PACK], BF16)
        gain_sb = tile("gain_sb", [P, HALVES, PACK], BF16)
        gain32 = tile("gain32", [P, HALVES, PACK], F32)
        y = tiles("y", UNITS, [P, PACK, CH], F32)
        y_il = tiles("y_il", 2, [P, PACK * CH], BF16)
        y_codes = tile("y_codes", [P, HALVES, M], U32)
        y_sc = tile("y_sc", [P, HALVES, M], U8)
        y_out = tiles("y_out", 2, [P, TILES, HALF], F32)
        u_exp = y_out[1][:].rearrange("p g (j c) -> p g j c", j=TILES)
        v_exp = y_out[0][:, 0:2, :].rearrange("p a (b e c) -> p (a b) e c", e=2, c=P)
        w_raw = y[UNITS - 1][:].bitcast(BF16)

        u_rows = out_0[M - V_PARK_ROWS - U_PARK_ROWS : M - V_PARK_ROWS, :]
        u_park = u_rows.rearrange("r n -> (r n)").rearrange("(c f) -> c f", c=2)
        v_park = out_0[M - V_PARK_ROWS : M, :].rearrange("r n -> (r n)")

        def load_x(c):
            rows = x[c * CH : (c + 1) * CH, :].rearrange("(a p j) d -> p a j d", a=2, j=2)
            nc.sync.dma_start(out=x_raw[c][:].rearrange("p (a j) d -> p a j d", a=2), in_=rows)

        def load_first_uv():
            rows = v[0:CH, :].rearrange("(a p j) i -> p a j i", a=2, j=2)
            nc.sync.dma_start(out=v_first[:].rearrange("p (a j) i -> p a j i", a=2), in_=rows)
            nc.sync.dma_start(out=u_first[:], in_=u[0:CH, :].rearrange("(j p) i -> p j i", p=P))

        def load_late_uv():
            nc.sync.dma_start(out=v_late[:], in_=v[CH:M, :].rearrange("(j p) i -> p j i", p=P))
            nc.sync.dma_start(out=u_late[:], in_=u[CH:M, :].rearrange("(a p j) i -> p a j i", a=4, j=2))

        def load_core(g):
            words = core_words[g : g + 1].rearrange("g p b -> p g b")
            nc.sync.dma_start(out=core_raw[:, g : g + 1, :].bitcast(I32), in_=words.bitcast(I32))

        def load_core_scales():
            for h in range(HALVES):
                rows = core_scales[:, :, h * HALF : (h + 1) * HALF].rearrange("g q n -> q g n")
                nc.sync.dma_start(out=cs_raw[h:P:2, :].bitcast(I32), in_=rows.bitcast(I32))

        def load_u_rep(c, g0, g1):
            rows = u_park[c - 1].rearrange("(i f) -> i f", i=16)[:, g0 * CH : g1 * CH]
            dst = u_rep[c % 2][:, g0:g1, :].rearrange("p g m -> p (g m)")
            nc.sync.dma_start(out=dst, in_=rows.unsqueeze(1).to_broadcast([16, 8, (g1 - g0) * CH]))

        def load_v_rep(c):
            rows = v_park[(c - 1) * 16 * CH : c * 16 * CH].rearrange("(q f) -> q f", q=8)
            nc.sync.dma_start(out=v_rep[c % 2][:], in_=rows.unsqueeze(0).to_broadcast([16, 8, 2 * CH]))

        def expand_v():
            words = v_first[:].bitcast(F32).rearrange("p j (q e) -> p j e q", e=2)
            nc.vector.tensor_copy(
                out=v_exp[:].rearrange("p j e (r q) -> p j e r q", q=8),
                in_=words.unsqueeze(3).to_broadcast([P, TILES, 2, 16, 8]),
            )

        def turn_words(words, b0):
            for j in range(TILES):
                for e in range(2):
                    col = (2 * (j % 2) + e) * P
                    nc.tensor.transpose(bank[b0 + j // 2][:, col : col + P], words(j, e), ident[:])

        def copy_words(dst, b0):
            dst = dst.rearrange("p (a m r) -> p a m r", a=2, r=4)
            for a in range(2):
                nc.scalar.copy(out=dst[:, a], in_=bank[b0 + a][:].rearrange("p (r m) -> p m r", r=4))

        def double_u():
            nc.vector.tensor_copy(
                out=u_dup[:].bitcast(BF16).rearrange("p j (i d) -> p j i d", d=2),
                in_=u_first[:].unsqueeze(3).to_broadcast([P, TILES, I, 2]),
            )

        def expand_u(g):
            nc.vector.tensor_copy(
                out=u_exp[:, g].rearrange("p j (i r) -> p j i r", r=8),
                in_=u_dup[:, :, 16 * g : 16 * g + 16].unsqueeze(3).to_broadcast([P, TILES, 16, 8]),
            )

        def turn_u(g, b):
            for j in range(TILES):
                nc.tensor.transpose(bank[b][:, j * P : (j + 1) * P], u_exp[:, g, j, :], ident[:])

        def order_v():
            words = v_late[:].bitcast(F32).rearrange("p (c j) (q e) -> p e c q j", j=TILES, e=2)
            for e in range(2):
                nc.scalar.copy(out=v_in[:, e, 0:64].rearrange("p (c q j) -> p c q j", c=2, j=TILES), in_=words[:, e])

        def order_u(c):
            for j in range(2):
                src = u_late[:, 2 * c - 2 : 2 * c, j, :].rearrange("p a (g i) -> p i g a", i=16)
                dst = u_in[:, c - 1, j, :].bitcast(BF16).rearrange("p (i g a d) -> p i g a d", g=PASSES, a=2, d=2)
                nc.scalar.copy(out=dst, in_=src.unsqueeze(4).to_broadcast([P, 16, PASSES, 2, 2]))

        def turn_late_v(b):
            for e in range(2):
                nc.tensor.transpose(bank[b][:, e * P : (e + 1) * P], v_in[:, e, :], ident[:])

        def turn_late_u(b):
            for k in range(4):
                nc.tensor.transpose(bank[b][:, k * P : (k + 1) * P], u_in[:, k // 2, k % 2, :], ident[:])

        def park_v(b):
            nc.scalar.copy(out=v_stage[0:64], in_=bank[b][0:64, 0:256].rearrange("p (e m) -> p m e", e=2))
            nc.sync.dma_start(out=v_park.rearrange("(p f) -> p f", p=64), in_=v_stage[0:64].rearrange("p m e -> p (m e)"))

        def park_u(b):
            nc.scalar.copy(
                out=u_stage[:].rearrange("p c (m j) -> p c m j", j=2),
                in_=bank[b][:].rearrange("p (c j m) -> p c m j", c=2, j=2),
            )
            nc.sync.dma_start(out=u_park.rearrange("c (p f) -> p c f", p=P), in_=u_stage[:])

        def permute_core(g, h):
            cols = slice(2 * h * HALF, 2 * (h + 1) * HALF)
            nc.vector.tensor_copy(
                out=core[:, g, cols].rearrange("p (t m b) -> p t m b", t=PACK, b=2),
                in_=core_raw[:, g, cols].rearrange("p (m t b) -> p t m b", t=PACK, b=2),
            )

        def permute_core_scales():
            nc.vector.tensor_copy(
                out=cs_perm[:].rearrange("p (t m) -> p t m", t=PACK),
                in_=cs_raw[:].rearrange("p (m t) -> p t m", t=PACK),
            )
            for q in range(4):
                nc.scalar.dma_start(out=cs[32 * q : 32 * q + 4].bitcast(I32), in_=cs_perm[32 * q : 32 * q + 32, :].bitcast(I32))

        def interleave_w(h):
            nc.scalar.copy(
                out=w_il[h][:].rearrange("p (t m j) -> p t m j", t=PACK, j=PACK),
                in_=w_raw[:, :, h * HALF : (h + 1) * HALF].rearrange("p j (m t) -> p t m j", t=PACK),
            )

        def quantize(codes, scales, src):
            nc.vector.quantize_mx(out=codes.bitcast(FP8X4), scales=scales, in_=src)

        def quant_w(h):
            quantize(w_codes[h][:], w_sc[h][:], w_il[h][:])

        def turn_x(c, b0):
            words = x_raw[c][:].bitcast(F32)
            turn_words(lambda j, e: words[:, j, e : 2 * P : 2], b0)
            copy_words(x_il[c % 2][:].bitcast(F32), b0)

        def quant_x(c):
            quantize(x_codes[c][:], x_sc[c][:], x_il[c % 2][:])

        def mult_z(c, g, u_words):
            pairs = u_words.bitcast(BF16).rearrange("p (m d) -> p m d", d=2)
            nc.vector.tensor_tensor(
                out=z[(PASSES * c + g) % Z_BUFS][:].rearrange("p (m e d) -> p m e d", e=2, d=2),
                in0=v_rep[c % 2][:].bitcast(BF16).rearrange("p (m e d) -> p m e d", e=2, d=2),
                in1=pairs.unsqueeze(2).to_broadcast([P, CH, 2, 2]),
                op=MULT,
            )

        def mult_z_sbuf(c, g):
            mult_z(c, g, u_rep[c % 2][:, g, :])

        def quant_z(c, g):
            quantize(z_codes[c % 2][:, g, :], z_sc[c % 2][:, g, :], z[(PASSES * c + g) % Z_BUFS][:])

        def mm_core(n, t, g, b, start, stop, m0=0, m1=CH):
            c, h = divmod(n, HALVES)
            col = h * HALF + t * P
            nc.tensor.matmul_mx(
                out=bank[b][:, m0:m1],
                lhsT=core[:, g, 2 * col : 2 * (col + P)].bitcast(FP4X4),
                lhsT_scale=cs[:, g, col : col + P],
                rhs=z_codes[c % 2][:, g, m0:m1].bitcast(FP8X4),
                rhs_scale=z_sc[c % 2][:, g, m0:m1],
                start=start,
                stop=stop,
            )

        def mm_x(n, t, b, start, stop, m0=0, m1=CH):
            c, h = divmod(n, HALVES)
            nc.tensor.matmul_mx(
                out=bank[b][:, m0:m1],
                lhsT=w_codes[h][:, t * P : (t + 1) * P].bitcast(FP8X4),
                lhsT_scale=w_sc[h][:, t * P : (t + 1) * P],
                rhs=x_codes[c][:, m0:m1].bitcast(FP8X4),
                rhs_scale=x_sc[c][:, m0:m1],
                start=start,
                stop=stop,
            )

        def tanh(n, t, b, m0=0, m1=CH):
            nc.scalar.activation(out=y[n][:, t, m0:m1], in_=bank[b][:, m0:m1], func=TANH, bias=bias_sb[:, n % HALVES, t : t + 1])

        def group(n, t, b, m0=0, m1=CH):
            mm_x(n, t, b, True, False, m0, m1)
            for g in range(PASSES):
                mm_core(n, t, g, b, False, g == PASSES - 1, m0, m1)
            tanh(n, t, b, m0, m1)

        def gain_on_scalar(n, t):
            nc.scalar.activation(out=y[n][:, t, :], in_=y[n][:, t, :], func=COPY, scale=gain32[:, n % HALVES, t : t + 1])

        def gain_on_vector(n, t, m0=0, m1=CH):
            rows = y[n][:, t, m0:m1]
            nc.vector.tensor_scalar(out=rows, in0=rows, scalar1=gain_sb[:, n % HALVES, t : t + 1], scalar2=None, op0=MULT)

        def interleave_y(n, m0=0, m1=CH):
            nc.vector.tensor_copy(
                out=y_il[n % 2][:, PACK * m0 : PACK * m1].rearrange("p (m t) -> p m t", t=PACK),
                in_=y[n][:, :, m0:m1].rearrange("p t m -> p m t"),
            )

        def quant_y(n, m0=0, m1=CH):
            c, h = divmod(n, HALVES)
            cols = slice(c * CH + m0, c * CH + m1)
            quantize(y_codes[:, h, cols], y_sc[:, h, cols], y_il[n % 2][:, PACK * m0 : PACK * m1])

        def store_words(n):
            c, h = divmod(n, HALVES)
            cols = slice(c * CH, (c + 1) * CH)
            dst = out_1[h, :, cols, :].rearrange("p m t -> p (m t)")
            nc.sync.dma_start(out=dst.bitcast(I32), in_=y_codes[:, h, cols].bitcast(I32))

        def store_scales(c0, c1):
            cols = slice(c0 * CH, c1 * CH)
            for q in range(4):
                dst = out_2[:, 4 * q : 4 * q + 4, cols].rearrange("h r m -> r h m")
                nc.sync.dma_start(out=dst.bitcast(I32), in_=y_sc[32 * q : 32 * q + 4, :, cols].bitcast(I32))

        def turn_y(n, j0, j1):
            for j in range(j0, j1):
                for t in range(PACK):
                    nc.tensor.transpose(bank[OUT_BANK + j][:, t * P : (t + 1) * P], y[n][:, t, j * P : (j + 1) * P], ident[:])

        def copy_y(n, j, copy):
            copy(
                out=y_out[n % 2][:, j, :].rearrange("m (p t) -> m p t", t=PACK),
                in_=bank[OUT_BANK + j][:].rearrange("m (t p) -> m p t", t=PACK),
            )

        def store_y(n, j0, j1):
            c, h = divmod(n, HALVES)
            rows = out_0[c * CH + j0 * P : c * CH + j1 * P, h * HALF : (h + 1) * HALF]
            nc.sync.dma_start(out=rows.rearrange("(j m) n -> m j n", m=P), in_=y_out[n % 2][:, j0:j1, :])

        def empty_out_banks(n):
            for j in range(TILES):
                copy_y(n, j, nc.scalar.copy)

        with tc.manual_schedule():
            nc.vector.memset(cs[:].rearrange("p g n -> p (g n)").bitcast(I32), 0)
            make_identity(nc, ident[:])
            nc.scalar.activation(out=v_in[:, :, 64:P], in_=ident[:].rearrange("p (e c) -> p e c", e=2), func=TANH)
            load_first_uv()
            load_core_scales()
            load_core(0)
            load_late_uv()
            load_x(0)
            load_core(1)

            expand_v()
            double_u()
            permute_core_scales()
            turn_words(lambda j, e: v_exp[:, j, e, :], 5)
            copy_words(v_rep[0][:], 5)
            nc.sync.dma_start(out=w_raw, in_=w.rearrange("(p j) n -> p j n", j=PACK))
            load_core(2)
            expand_u(0)
            expand_u(1)
            permute_core(0, 0)
            expand_u(2)
            expand_u(3)
            turn_u(0, 0)
            turn_u(1, 7)
            order_v()
            order_u(1)
            order_u(2)
            turn_u(2, 1)
            turn_u(3, 2)
            turn_late_v(3)
            turn_late_u(4)
            mult_z(0, 0, bank[0][:])
            permute_core(0, 1)
            quant_z(0, 0)
            for g in (2, 3):
                nc.scalar.copy(out=u_rep[0][:, g, :], in_=bank[g - 1][:])
            park_v(3)
            park_u(4)
            for b in range(5):
                mm_core(b // PACK, b % PACK, 0, b, True, False)
            turn_x(0, 5)
            load_core(3)
            nc.sync.dma_start(out=bias_sb[:], in_=bias.rearrange("(h p t) -> p h t", h=HALVES, t=PACK))
            nc.sync.dma_start(out=gain_sb[:], in_=gain.rearrange("(h p t) -> p h t", h=HALVES, t=PACK))
            load_v_rep(1)
            load_u_rep(1, 0, 1)
            load_u_rep(1, 1, 2)
            load_u_rep(1, 2, PASSES)
            load_x(1)
            interleave_w(0)
            interleave_w(1)
            nc.scalar.copy(out=gain32[:], in_=gain_sb[:])

            mult_z(0, 1, bank[7][:])
            permute_core(1, 0)
            quant_z(0, 1)
            permute_core(1, 1)
            mult_z_sbuf(0, 2)
            permute_core(2, 0)
            quant_z(0, 2)
            permute_core(2, 1)
            mult_z_sbuf(0, 3)
            quant_x(0)
            quant_w(0)
            permute_core(3, 0)
            quant_z(0, 3)
            permute_core(3, 1)
            mult_z_sbuf(1, 0)
            quant_w(1)
            quant_z(1, 0)
            mm_core(1, 3, 0, 7, True, False)
            for b in (0, 1, 2, 3, 4, 7):
                mm_core(b // PACK, b % PACK, 1, b, False, False)
            for g in (0, 1):
                for b in (5, 6):
                    mm_core(1, b % PACK, g, b, g == 0, False)
            for b in range(2 * PACK):
                mm_core(b // PACK, b % PACK, 2, b, False, False)
            for t in range(PACK):
                mm_x(0, t, t, False, False)
            for t in range(PACK):
                mm_core(0, t, PASSES - 1, t, False, True)
                tanh(0, t, t)
            for t in range(PACK):
                mm_core(1, t, PASSES - 1, PACK + t, False, False)
            load_v_rep(2)
            load_u_rep(2, 0, 1)
            load_u_rep(2, 1, PASSES)
            load_x(2)
            mult_z_sbuf(1, 1)
            mult_z_sbuf(1, 2)
            quant_z(1, 1)
            for t in range(PACK):
                mm_x(1, t, PACK + t, False, True)
                tanh(1, t, PACK + t)
            mult_z_sbuf(1, 3)
            quant_z(1, 2)

            for t in range(PACK):
                mm_core(2, t, 0, t, True, False)
            turn_x(1, OUT_BANK)
            quant_z(1, 3)
            quant_x(1)
            for t in range(PACK):
                gain_on_scalar(0, t)
            for g in range(1, PASSES):
                for t in range(PACK):
                    mm_core(2, t, g, t, False, False)
            for t in range(PACK):
                mm_x(2, t, t, False, True)
                tanh(2, t, t)
            turn_y(0, 0, TILES)
            for t in range(PACK):
                gain_on_vector(1, t)
            mult_z_sbuf(2, 0)
            for g in range(1, PASSES):
                mult_z_sbuf(2, g)
                quant_z(2, g - 1)
            empty_out_banks(0)
            store_y(0, 0, TILES)

            for t in (0, 1):
                group(3, t, t)
            turn_x(2, 2)
            turn_y(1, 0, TILES)
            gain_on_vector(2, 0)
            quant_z(2, PASSES - 1)
            for t in range(1, PACK):
                gain_on_vector(2, t)
            empty_out_banks(1)
            quant_x(2)
            store_y(1, 0, TILES)
            interleave_y(0)
            for t in (2, 3):
                group(3, t, t)
            turn_y(2, 0, TILES)
            for t in range(PACK - 1):
                gain_on_vector(3, t)
            quant_y(0)
            store_words(0)
            empty_out_banks(2)
            gain_on_vector(3, PACK - 1)
            store_y(2, 0, TILES)

            for t in (0, 1):
                group(4, t, t)
            turn_y(3, 0, TILES)
            empty_out_banks(3)
            store_y(3, 0, TILES)
            interleave_y(1)
            interleave_y(2)
            quant_y(1)
            quant_y(2)
            interleave_y(3)
            store_words(1)
            store_words(2)
            for t in (2, 3):
                group(4, t, t)
            for t in range(PACK - 1):
                gain_on_vector(4, t)
            quant_y(3)
            gain_on_vector(4, PACK - 1)
            store_words(3)
            store_scales(0, 2)

            last = UNITS - 1
            group(last, 0, 0)
            turn_y(4, 0, TILES)
            interleave_y(4)
            gain_on_vector(last, 0)
            quant_y(4)
            empty_out_banks(4)
            store_words(4)
            store_y(4, 0, TILES)
            group(last, 1, 1)
            gain_on_vector(last, 1)

            for j in range(TILES):
                for t in (2, 3):
                    group(last, t, (2 * j + t) % PACK, j * P, (j + 1) * P)
                    gain_on_vector(last, t, j * P, (j + 1) * P)
                if j == TILES - 2:
                    turn_y(last, 0, 2)
                    copy_y(last, 0, nc.scalar.copy)
                    copy_y(last, 1, nc.vector.tensor_copy)
                    store_y(last, 0, 2)
                    interleave_y(last, 0, CH // 2)
            turn_y(last, 2, TILES)
            quant_y(last, 0, CH // 2)
            interleave_y(last, CH // 2, CH)
            copy_y(last, 2, nc.scalar.copy)
            store_y(last, 2, 3)
            quant_y(last, CH // 2, CH)
            copy_y(last, 3, nc.scalar.copy)
            store_y(last, 3, TILES)
            store_scales(2, CHUNKS)
            store_words(last)
